import numpy as np
import ml_dtypes


def mxq(x, axis, fmt="e4m3"):
    dtype, down = {"e4m3": (ml_dtypes.float8_e4m3fn, 7), "e5m2": (ml_dtypes.float8_e5m2, 14)}[fmt]
    v = np.moveaxis(np.asarray(x, np.float32).astype(ml_dtypes.bfloat16).astype(np.float64), axis, -1)
    blocks = v.reshape(v.shape[:-1] + (-1, 32))
    amax = np.abs(blocks).max(-1, keepdims=True)
    byte = np.maximum(np.where(amax > 0, np.frexp(amax)[1] - 1 + 127, 0) - down, 1)
    scale = np.exp2(byte - 127.0)
    codes = (blocks / scale).astype(np.float32).astype(dtype).astype(np.float64)
    return np.moveaxis((codes * scale).reshape(v.shape), -1, axis)


WIDE = False


def mx_kscale(k):
    if not WIDE:
        return np.ones(k)
    levels = np.array([10, -10, 5, -5, 0])
    if k % 512:
        return np.exp2(np.random.permutation(np.resize(levels, k // 32))).repeat(32)
    a = np.empty((k // 512, 16))
    for p in range(k // 512):
        a[p, :8] = np.random.permutation(np.resize(levels, 8))
        for g in range(8):
            far = levels[np.abs(levels - a[p, g]) >= 10]
            a[p, g + 8] = far[np.random.randint(len(far))]
    return np.exp2(a.ravel()).repeat(32)


def f64(x):
    return np.asarray(x).astype(np.float64)


def striped(idx):
    return np.tile(idx.reshape(-1, 16).T, (8, 1)).astype(np.uint16)


def unstriped(offs):
    return offs[:16].T.reshape(-1).astype(np.int64)


def striped8(idx):
    return np.concatenate([x.reshape(-1, 16).T for x in idx]).astype(np.uint16)


def runs(offs, k):
    lists = np.stack([offs[16 * r : 16 * r + 16].T.reshape(-1) for r in range(8)]).astype(np.int64)
    return lists[np.arange(k) % 512 // 64]


def pack_weight(w):
    k, n = w.shape
    w = f64(np.asarray(w, np.float32).astype(ml_dtypes.bfloat16)).reshape(k // 32, 32, n)
    amax = np.abs(w).max(1)
    byte = np.clip(np.where(amax > 0, np.frexp(amax)[1] - 1 + 127 - 7, 1), 1, 254)
    scaled = (w * np.exp2(127.0 - byte)[:, None, :]).reshape(k, n).astype(np.float32)
    words = np.ascontiguousarray(scaled.reshape(k // 512, 128, 4, n).transpose(0, 1, 3, 2)).astype(ml_dtypes.float8_e4m3fn).view(np.uint8)
    return words, np.ascontiguousarray(byte.astype(np.uint8).reshape(k // 512, 16, n))


def unpack_weight(words, scales):
    g, p, n, _ = words.shape
    vals = np.ascontiguousarray(words).view(ml_dtypes.float8_e4m3fn).astype(np.float64) * np.repeat(np.exp2(scales.astype(np.float64) - 127.0), 8, axis=1)[..., None]
    return vals.transpose(0, 1, 3, 2).reshape(g * 512, n)


K, T, S, H, N, V = 512, 2048, 1024, 512, 256, 512


def setup_inputs():
    n = np.random.standard_normal
    s = mx_kscale(K)[:, None]
    u = mx_kscale(H)
    packed_xT = pack_weight(n((K, T)) * s)
    packed_w2 = pack_weight(n((H, N)) / np.sqrt(H) / u[:, None])
    return {
        "x_words": packed_xT[0],
        "x_scales": packed_xT[1],
        "w1": (n((K, H)) / np.sqrt(K) / s * u).astype(np.float32),
        "w2_words": packed_w2[0],
        "w2_scales": packed_w2[1],
        "offs": striped8(np.stack([np.random.permutation(T)[:S] for _ in range(8)])),
        "left": striped(np.random.permutation(S)[:V]),
        "right": striped(np.random.permutation(S)[:V]),
    }


def reference(x_words, x_scales, w1, w2_words, w2_scales, offs, left, right):
    xq = unpack_weight(x_words, x_scales)[np.arange(K)[:, None], runs(offs, K)]
    h = mxq(f64(w1), 0, "e4m3").T @ xq
    z = np.abs(h[:, unstriped(left)] - h[:, unstriped(right)])
    return unpack_weight(w2_words, w2_scales).T @ mxq(z, 0, "e4m3")

@@ -1,0 +1,191 @@
+from contextlib import ExitStack
+
+import concourse.mybir as mybir
+
+K, T, S, H, N, V = 512, 2048, 1024, 512, 256, 512
+FLOPS = 2 * K * H * S + 2 * H * N * V
+
+F32 = mybir.dt.float32
+BF16 = mybir.dt.bfloat16
+I32 = mybir.dt.int32
+U32 = mybir.dt.uint32
+U16 = mybir.dt.uint16
+U8 = mybir.dt.uint8
+FP8X4 = mybir.dt.float8_e4m3fn_x4
+ABS = mybir.ActivationFunctionType.Abs
+SUB = mybir.AluOpType.subtract
+
+P = 128
+BANK = 512
+CHUNKS = [(0, 256), (256, 384), (384, 512)]
+
+
+def tile_picked_phpair_abs_p_kernel(
+    tc, x_words, x_scales, w1, w2_words, w2_scales, offs, left, right, out
+):
+    nc = tc.nc
+    with ExitStack() as ctx:
+        keep = ctx.enter_context(tc.tile_pool(name="keep", bufs=1))
+        psum = ctx.enter_context(tc.psum_pool(name="psum", bufs=1))
+
+        offs_sb = keep.tile([P, S // 16], U16, name="offs_sb")
+        left_sb = keep.tile([P, V // 16], U16, name="left_sb")
+        right_sb = keep.tile([P, V // 16], U16, name="right_sb")
+
+        nc.sync.dma_start(offs_sb[:], offs)
+        xs_all = keep.tile([P, T], U8, name="xs_all", tag="xs_then_w2", align_bytes=64)
+        nc.scalar.dma_start(
+            xs_all[:].bitcast(I32), x_scales[0].bitcast(I32).unsqueeze(1).to_broadcast([16, 8, T // 4])
+        )
+        xw_all = keep.tile([P, T], U32, name="xw_all", align_bytes=64)
+        nc.sync.dma_start(xw_all[:].bitcast(I32), x_words[0].rearrange("p n t -> p (n t)").bitcast(I32))
+        w1_rows = w1.rearrange("(p j) c -> p j c", j=4)
+        w1_raw = [keep.tile([P, 2, H], F32, name="w1_raw%d" % a) for a in range(2)]
+        for a in range(2):
+            nc.sync.dma_start(w1_raw[a][:], w1_rows[:, 2 * a : 2 * a + 2, :])
+        nc.sync.dma_start(left_sb[:], left)
+        nc.sync.dma_start(right_sb[:], right)
+
+        warm = keep.tile([P, 2], F32, name="warm")
+        nc.vector.memset(warm[:, 0:1], 0.0)
+        nc.scalar.activation(warm[:, 1:2], warm[:, 0:1], ABS)
+
+        xs = keep.tile([P, S], U8, name="xs", align_bytes=64)
+        nc.gpsimd.memset(xs[:].bitcast(I32), 0)
+        w2s = keep.tile([P, N], U8, name="w2s", align_bytes=64)
+        nc.gpsimd.memset(w2s[:].bitcast(I32), 0)
+        for q in range(4):
+            nc.gpsimd.dma_start(
+                w2s[32 * q : 32 * q + 4, :].bitcast(I32), w2_scales[0, 4 * q : 4 * q + 4, :].bitcast(I32)
+            )
+
+        xs_picked = keep.tile([P, S], U8, name="xs_picked", align_bytes=64)
+        nc.vector.tensor_copy(xs_picked[:], xs_all[:].indirect(offs_sb[:]))
+        for r in range(4):
+            nc.scalar.dma_start(xs[r:P:32, :].bitcast(I32), xs_picked[8 * r : P : 32, :].bitcast(I32))
+        w2w = keep.tile([P, N], U32, name="w2w", tag="xs_then_w2", align_bytes=64)
+        nc.sync.dma_start(w2w[:].bitcast(I32), w2_words[0].rearrange("p n t -> p (n t)").bitcast(I32))
+
+        xw = keep.tile([P, S], U32, name="xw", align_bytes=64)
+        nc.vector.tensor_copy(xw[:], xw_all[:].indirect(offs_sb[:]))
+
+        w1_bf = [keep.tile([P, 2 * P * 4], BF16, name="w1_bf%d" % b, align_bytes=64) for b in range(2)]
+
+        def cast(copy, a, b):
+            copy(
+                w1_bf[b][:].rearrange("p (t m j) -> p m t j", t=2, j=4)[:, :, :, 2 * a : 2 * a + 2],
+                w1_raw[a][:].rearrange("p j (m t) -> p m t j", t=4)[:, :, 2 * b : 2 * b + 2, :],
+            )
+
+        cast(nc.scalar.copy, 0, 0)
+        cast(nc.scalar.copy, 0, 1)
+        cast(nc.vector.tensor_copy, 1, 0)
+
+        w1w = [keep.tile([P, P], U32, name="w1w%d" % t, align_bytes=64) for t in range(4)]
+        w1s = [keep.tile([P, P], U8, name="w1s%d" % t, align_bytes=64) for t in range(4)]
+        h = [keep.tile([P, S], F32, name="h%d" % t) for t in range(4)]
+
+        def quantize_w1(t):
+            nc.vector.quantize_mx(
+                out=w1w[t][:].bitcast(FP8X4),
+                scales=w1s[t][:],
+                in_=w1_bf[t // 2][:, (t % 2) * 4 * P : (t % 2 + 1) * 4 * P],
+            )
+
+        def project(t, a, b, bank, copy):
+            acc = psum.tile([P, b - a], F32, name="acc", tag="bank%d" % bank)
+            nc.tensor.matmul_mx(
+                out=acc[:],
+                lhsT=w1w[t][:].bitcast(FP8X4),
+                lhsT_scale=w1s[t][:],
+                rhs=xw[:, a:b].bitcast(FP8X4),
+                rhs_scale=xs[:, a:b],
+                start=True,
+                stop=True,
+            )
+            copy(h[t][:, a:b], acc[:])
+
+        quantize_w1(0)
+        quantize_w1(1)
+        for u in range(4):
+            project(0, 256 * u, 256 * (u + 1), u, nc.vector.tensor_copy if u % 2 else nc.scalar.copy)
+        cast(nc.vector.tensor_copy, 1, 1)
+        quantize_w1(2)
+        quantize_w1(3)
+        for t in range(1, 4):
+            for u in range(2):
+                project(t, BANK * u, BANK * (u + 1), (2 * t + 2 + u) % 8, nc.scalar.copy)
+
+        z = [keep.tile([P, 4 * (b - a)], BF16, name="z%d" % c, align_bytes=64) for c, (a, b) in enumerate(CHUNKS)]
+        out_rows = out.rearrange("(a p) v -> p a v", p=P)
+
+        def fetch_left(dst, t, a, b):
+            nc.vector.tensor_copy(dst, h[t][:].indirect(left_sb[:, a // 16 : b // 16]))
+
+        def fetch_right(dst, t, a, b, picked):
+            nc.vector.tensor_tensor(dst, h[t][:].indirect(right_sb[:, a // 16 : b // 16]), picked, SUB)
+
+        def take_abs(c, pair, src):
+            nc.scalar.activation(
+                z[c][:].rearrange("p (v t) -> p v t", t=4)[:, :, 2 * pair : 2 * pair + 2],
+                src.rearrange("p t v -> p v t"),
+                ABS,
+            )
+
+        zw = [keep.tile([P, b - a], U32, name="zw%d" % a, align_bytes=64) for a, b in CHUNKS]
+        zs = [keep.tile([P, b - a], U8, name="zs%d" % a, align_bytes=64) for a, b in CHUNKS]
+
+        def quantize_z(c):
+            nc.vector.quantize_mx(out=zw[c][:].bitcast(FP8X4), scales=zs[c][:], in_=z[c][:])
+
+        def finish(c, copy):
+            a, b = CHUNKS[c]
+            res = psum.tile([P, 2, b - a], F32, name="res", tag="bank%d" % (2 + c))
+            for m in range(2):
+                nc.tensor.matmul_mx(
+                    out=res[:, m, :],
+                    lhsT=w2w[:, m * P : (m + 1) * P].bitcast(FP8X4),
+                    lhsT_scale=w2s[:, m * P : (m + 1) * P],
+                    rhs=zw[c][:].bitcast(FP8X4),
+                    rhs_scale=zs[c][:],
+                    start=True,
+                    stop=True,
+                )
+            staged = keep.tile([P, 2, b - a], F32, name="staged%d" % c)
+            copy(staged[:], res[:])
+            nc.sync.dma_start(out_rows[:, :, a:b], staged[:])
+
+        half = V // 2
+        d01 = [keep.tile([P, 2, half], F32, name="d01", tag="pair%d" % u) for u in range(2)]
+        for t in range(2):
+            picked = [keep.tile([P, half], F32, name="left%d_%d" % (t, u)) for u in range(2)]
+            for u in range(2):
+                fetch_left(picked[u][:], t, half * u, half * (u + 1))
+            for u in range(2):
+                fetch_right(d01[u][:, t, :], t, half * u, half * (u + 1), picked[u][:])
+        for c, (a, b) in enumerate(CHUNKS):
+            take_abs(c, 0, d01[a // half][:, :, a % half : a % half + b - a])
+
+        def fetch_left23(u, tag):
+            picked = keep.tile([P, 2, half], F32, name="left23", tag=tag)
+            for t in (2, 3):
+                fetch_left(picked[:, t - 2, :], t, half * u, half * (u + 1))
+            return picked
+
+        def fetch_chunk(c, picked, tag):
+            a, b = CHUNKS[c]
+            d23 = keep.tile([P, 2, b - a], F32, name="d23", tag=tag)
+            for t in (2, 3):
+                fetch_right(d23[:, t - 2, :], t, a, b, picked[:, t - 2, a % half : a % half + b - a])
+            take_abs(c, 1, d23[:])
+
+        fetch_chunk(0, fetch_left23(0, "left23"), "pair0")
+        picked = fetch_left23(1, "pair1")
+        fetch_chunk(1, picked, "d23")
+        quantize_z(0)
+        fetch_chunk(2, picked, "pair0")
+        quantize_z(1)
+        quantize_z(2)
+        finish(0, nc.scalar.copy)
+        finish(1, nc.scalar.copy)
+        finish(2, nc.vector.tensor_copy)

@@ -34,7 +34,7 @@ def tile_picked_phpair_abs_p_kernel(
 
         nc.sync.dma_start(offs_sb[:], offs)
         xs_all = keep.tile([P, T], U8, name="xs_all", tag="xs_then_w2", align_bytes=64)
-        nc.scalar.dma_start(
+        nc.sync.dma_start(
             xs_all[:].bitcast(I32), x_scales[0].bitcast(I32).unsqueeze(1).to_broadcast([16, 8, T // 4])
         )
         xw_all = keep.tile([P, T], U32, name="xw_all", align_bytes=64)
@@ -52,12 +52,6 @@ def tile_picked_phpair_abs_p_kernel(
 
         xs = keep.tile([P, S], U8, name="xs", align_bytes=64)
         nc.gpsimd.memset(xs[:].bitcast(I32), 0)
-        w2s = keep.tile([P, N], U8, name="w2s", align_bytes=64)
-        nc.gpsimd.memset(w2s[:].bitcast(I32), 0)
-        for q in range(4):
-            nc.gpsimd.dma_start(
-                w2s[32 * q : 32 * q + 4, :].bitcast(I32), w2_scales[0, 4 * q : 4 * q + 4, :].bitcast(I32)
-            )
 
         xs_picked = keep.tile([P, S], U8, name="xs_picked", align_bytes=64)
         nc.vector.tensor_copy(xs_picked[:], xs_all[:].indirect(offs_sb[:]))
@@ -65,6 +59,12 @@ def tile_picked_phpair_abs_p_kernel(
             nc.scalar.dma_start(xs[r:P:32, :].bitcast(I32), xs_picked[8 * r : P : 32, :].bitcast(I32))
         w2w = keep.tile([P, N], U32, name="w2w", tag="xs_then_w2", align_bytes=64)
         nc.sync.dma_start(w2w[:].bitcast(I32), w2_words[0].rearrange("p n t -> p (n t)").bitcast(I32))
+        w2s = keep.tile([P, N], U8, name="w2s", tag="xs_picked", align_bytes=64)
+        nc.gpsimd.memset(w2s[:].bitcast(I32), 0)
+        for q in range(4):
+            nc.sync.dma_start(
+                w2s[32 * q : 32 * q + 4, :].bitcast(I32), w2_scales[0, 4 * q : 4 * q + 4, :].bitcast(I32)
+            )
 
         xw = keep.tile([P, S], U32, name="xw", align_bytes=64)
         nc.vector.tensor_copy(xw[:], xw_all[:].indirect(offs_sb[:]))

@@ -34,7 +34,7 @@ def tile_picked_phpair_abs_p_kernel(
 
         nc.sync.dma_start(offs_sb[:], offs)
         xs_all = keep.tile([P, T], U8, name="xs_all", tag="xs_then_w2", align_bytes=64)
-        nc.sync.dma_start(
+        nc.scalar.dma_start(
             xs_all[:].bitcast(I32), x_scales[0].bitcast(I32).unsqueeze(1).to_broadcast([16, 8, T // 4])
         )
         xw_all = keep.tile([P, T], U32, name="xw_all", align_bytes=64)
@@ -107,8 +107,8 @@ def tile_picked_phpair_abs_p_kernel(
 
         quantize_w1(0)
         quantize_w1(1)
-        for u in range(4):
-            project(0, 256 * u, 256 * (u + 1), u, nc.vector.tensor_copy if u % 2 else nc.scalar.copy)
+        for u, (a, b) in enumerate([(0, 512), (512, 768), (768, 896), (896, 1024)]):
+            project(0, a, b, u, nc.vector.tensor_copy if u % 2 else nc.scalar.copy)
         cast(nc.vector.tensor_copy, 1, 1)
         quantize_w1(2)
         quantize_w1(3)
@@ -138,22 +138,34 @@ def tile_picked_phpair_abs_p_kernel(
         def quantize_z(c):
             nc.vector.quantize_mx(out=zw[c][:].bitcast(FP8X4), scales=zs[c][:], in_=z[c][:])
 
+        def second_product(res, c, m):
+            nc.tensor.matmul_mx(
+                out=res,
+                lhsT=w2w[:, m * P : (m + 1) * P].bitcast(FP8X4),
+                lhsT_scale=w2s[:, m * P : (m + 1) * P],
+                rhs=zw[c][:].bitcast(FP8X4),
+                rhs_scale=zs[c][:],
+                start=True,
+                stop=True,
+            )
+
         def finish(c, copy):
             a, b = CHUNKS[c]
             res = psum.tile([P, 2, b - a], F32, name="res", tag="bank%d" % (2 + c))
             for m in range(2):
-                nc.tensor.matmul_mx(
-                    out=res[:, m, :],
-                    lhsT=w2w[:, m * P : (m + 1) * P].bitcast(FP8X4),
-                    lhsT_scale=w2s[:, m * P : (m + 1) * P],
-                    rhs=zw[c][:].bitcast(FP8X4),
-                    rhs_scale=zs[c][:],
-                    start=True,
-                    stop=True,
-                )
+                second_product(res[:, m, :], c, m)
             staged = keep.tile([P, 2, b - a], F32, name="staged%d" % c)
             copy(staged[:], res[:])
             nc.sync.dma_start(out_rows[:, :, a:b], staged[:])
+
+        def finish_split(c):
+            a, b = CHUNKS[c]
+            for m, copy in enumerate((nc.vector.tensor_copy, nc.scalar.copy)):
+                res = psum.tile([P, b - a], F32, name="res", tag="bank%d" % (4 + m))
+                second_product(res[:], c, m)
+                staged = keep.tile([P, b - a], F32, name="last%d" % m)
+                copy(staged[:], res[:])
+                nc.sync.dma_start(out_rows[:, m, a:b], staged[:])
 
         half = V // 2
         d01 = [keep.tile([P, 2, half], F32, name="d01", tag="pair%d" % u) for u in range(2)]
@@ -188,4 +200,4 @@ def tile_picked_phpair_abs_p_kernel(
         quantize_z(2)
         finish(0, nc.scalar.copy)
         finish(1, nc.scalar.copy)
-        finish(2, nc.vector.tensor_copy)
+        finish_split(2)

@@ -40,7 +40,7 @@ def tile_picked_phpair_abs_p_kernel(
         xw_all = keep.tile([P, T], U32, name="xw_all", align_bytes=64)
         nc.sync.dma_start(xw_all[:].bitcast(I32), x_words[0].rearrange("p n t -> p (n t)").bitcast(I32))
         w1_rows = w1.rearrange("(p j) c -> p j c", j=4)
-        w1_raw = [keep.tile([P, 2, H], F32, name="w1_raw%d" % a) for a in range(2)]
+        w1_raw = [keep.tile([P, 2, H], F32, name="w1_raw%d" % a, align_bytes=64) for a in range(2)]
         for a in range(2):
             nc.sync.dma_start(w1_raw[a][:], w1_rows[:, 2 * a : 2 * a + 2, :])
         nc.sync.dma_start(left_sb[:], left)
@@ -56,30 +56,36 @@ def tile_picked_phpair_abs_p_kernel(
         xs_picked = keep.tile([P, S], U8, name="xs_picked", align_bytes=64)
         nc.vector.tensor_copy(xs_picked[:], xs_all[:].indirect(offs_sb[:]))
         for r in range(4):
-            nc.scalar.dma_start(xs[r:P:32, :].bitcast(I32), xs_picked[8 * r : P : 32, :].bitcast(I32))
-        w2w = keep.tile([P, N], U32, name="w2w", tag="xs_then_w2", align_bytes=64)
-        nc.sync.dma_start(w2w[:].bitcast(I32), w2_words[0].rearrange("p n t -> p (n t)").bitcast(I32))
-        w2s = keep.tile([P, N], U8, name="w2s", tag="xs_picked", align_bytes=64)
-        nc.gpsimd.memset(w2s[:].bitcast(I32), 0)
-        for q in range(4):
-            nc.sync.dma_start(
-                w2s[32 * q : 32 * q + 4, :].bitcast(I32), w2_scales[0, 4 * q : 4 * q + 4, :].bitcast(I32)
-            )
+            queue = nc.sync if r % 2 else nc.scalar
+            queue.dma_start(xs[r:P:32, :].bitcast(I32), xs_picked[8 * r : P : 32, :].bitcast(I32))
 
         xw = keep.tile([P, S], U32, name="xw", align_bytes=64)
         nc.vector.tensor_copy(xw[:], xw_all[:].indirect(offs_sb[:]))
 
         w1_bf = [keep.tile([P, 2 * P * 4], BF16, name="w1_bf%d" % b, align_bytes=64) for b in range(2)]
 
-        def cast(copy, a, b):
+        def cast(copy, a, t0, t1):
             copy(
-                w1_bf[b][:].rearrange("p (t m j) -> p m t j", t=2, j=4)[:, :, :, 2 * a : 2 * a + 2],
-                w1_raw[a][:].rearrange("p j (m t) -> p m t j", t=4)[:, :, 2 * b : 2 * b + 2, :],
+                w1_bf[t0 // 2][:].rearrange("p (t m j) -> p m t j", t=2, j=4)[
+                    :, :, t0 % 2 : t0 % 2 + t1 - t0, 2 * a : 2 * a + 2
+                ],
+                w1_raw[a][:].rearrange("p j (m t) -> p m t j", t=4)[:, :, t0:t1, :],
             )
 
-        cast(nc.scalar.copy, 0, 0)
-        cast(nc.scalar.copy, 0, 1)
-        cast(nc.vector.tensor_copy, 1, 0)
+        cast(nc.scalar.copy, 0, 0, 2)
+        cast(nc.scalar.copy, 0, 2, 4)
+        cast(nc.vector.tensor_copy, 1, 0, 1)
+        cast(nc.vector.tensor_copy, 1, 1, 2)
+        cast(nc.scalar.copy, 1, 2, 4)
+
+        w2w = keep.tile([P, N], U32, name="w2w", tag="w1_raw0", align_bytes=64)
+        nc.sync.dma_start(w2w[:].bitcast(I32), w2_words[0].rearrange("p n t -> p (n t)").bitcast(I32))
+        w2s = keep.tile([P, N], U8, name="w2s", tag="xs_picked", align_bytes=64)
+        for q in range(4):
+            nc.sync.dma_start(
+                w2s[32 * q : 32 * q + 32, :].bitcast(I32),
+                w2_scales[0, 4 * q : 4 * q + 4, :].bitcast(I32).unsqueeze(0).to_broadcast([8, 4, N // 4]),
+            )
 
         w1w = [keep.tile([P, P], U32, name="w1w%d" % t, align_bytes=64) for t in range(4)]
         w1s = [keep.tile([P, P], U8, name="w1s%d" % t, align_bytes=64) for t in range(4)]
@@ -107,14 +113,13 @@ def tile_picked_phpair_abs_p_kernel(
 
         quantize_w1(0)
         quantize_w1(1)
-        for u, (a, b) in enumerate([(0, 512), (512, 768), (768, 896), (896, 1024)]):
-            project(0, a, b, u, nc.vector.tensor_copy if u % 2 else nc.scalar.copy)
-        cast(nc.vector.tensor_copy, 1, 1)
+        for u, (a, b) in enumerate([(0, 256), (256, 512), (512, 768), (768, 896), (896, 1024)]):
+            project(0, a, b, u, nc.vector.tensor_copy if u == 3 else nc.scalar.copy)
         quantize_w1(2)
         quantize_w1(3)
         for t in range(1, 4):
             for u in range(2):
-                project(t, BANK * u, BANK * (u + 1), (2 * t + 2 + u) % 8, nc.scalar.copy)
+                project(t, BANK * u, BANK * (u + 1), (2 * t + 3 + u) % 8, nc.scalar.copy)
 
         z = [keep.tile([P, 4 * (b - a)], BF16, name="z%d" % c, align_bytes=64) for c, (a, b) in enumerate(CHUNKS)]
         out_rows = out.rearrange("(a p) v -> p a v", p=P)
@@ -151,7 +156,7 @@ def tile_picked_phpair_abs_p_kernel(
 
         def finish(c, copy):
             a, b = CHUNKS[c]
-            res = psum.tile([P, 2, b - a], F32, name="res", tag="bank%d" % (2 + c))
+            res = psum.tile([P, 2, b - a], F32, name="res", tag="bank%d" % (3 + c))
             for m in range(2):
                 second_product(res[:, m, :], c, m)
             staged = keep.tile([P, 2, b - a], F32, name="staged%d" % c)
@@ -161,11 +166,11 @@ def tile_picked_phpair_abs_p_kernel(
         def finish_split(c):
             a, b = CHUNKS[c]
             for m, copy in enumerate((nc.vector.tensor_copy, nc.scalar.copy)):
-                res = psum.tile([P, b - a], F32, name="res", tag="bank%d" % (4 + m))
+                res = psum.tile([P, b - a], F32, name="res", tag="bank%d" % (5 + m))
                 second_product(res[:], c, m)
                 staged = keep.tile([P, b - a], F32, name="last%d" % m)
                 copy(staged[:], res[:])
-                nc.sync.dma_start(out_rows[:, m, a:b], staged[:])
+                (nc.scalar if m else nc.sync).dma_start(out_rows[:, m, a:b], staged[:])
 
         half = V // 2
         d01 = [keep.tile([P, 2, half], F32, name="d01", tag="pair%d" % u) for u in range(2)]

@@ -156,21 +156,21 @@ def tile_picked_phpair_abs_p_kernel(
 
         def finish(c, copy):
             a, b = CHUNKS[c]
-            res = psum.tile([P, 2, b - a], F32, name="res", tag="bank%d" % (3 + c))
+            res = psum.tile([P, 2, b - a], F32, name="res", tag="bank%d" % (4 + c))
             for m in range(2):
                 second_product(res[:, m, :], c, m)
             staged = keep.tile([P, 2, b - a], F32, name="staged%d" % c)
             copy(staged[:], res[:])
             nc.sync.dma_start(out_rows[:, :, a:b], staged[:])
 
-        def finish_split(c):
+        def finish_split(c, bank, queues):
             a, b = CHUNKS[c]
             for m, copy in enumerate((nc.vector.tensor_copy, nc.scalar.copy)):
-                res = psum.tile([P, b - a], F32, name="res", tag="bank%d" % (5 + m))
+                res = psum.tile([P, b - a], F32, name="res", tag="bank%d" % (bank + m))
                 second_product(res[:], c, m)
-                staged = keep.tile([P, b - a], F32, name="last%d" % m)
+                staged = keep.tile([P, b - a], F32, name="last%d_%d" % (c, m))
                 copy(staged[:], res[:])
-                (nc.scalar if m else nc.sync).dma_start(out_rows[:, m, a:b], staged[:])
+                queues[m].dma_start(out_rows[:, m, a:b], staged[:])
 
         half = V // 2
         d01 = [keep.tile([P, 2, half], F32, name="d01", tag="pair%d" % u) for u in range(2)]
@@ -203,6 +203,6 @@ def tile_picked_phpair_abs_p_kernel(
         fetch_chunk(2, picked, "pair0")
         quantize_z(1)
         quantize_z(2)
-        finish(0, nc.scalar.copy)
+        finish_split(0, 3, (nc.sync, nc.sync))
         finish(1, nc.scalar.copy)
-        finish_split(2)
+        finish_split(2, 6, (nc.sync, nc.scalar))

@@ -17,7 +17,12 @@ SUB = mybir.AluOpType.subtract
 
 P = 128
 BANK = 512
+QUARTER = S // 4
+
 CHUNKS = [(0, 256), (256, 384), (384, 512)]
+
+TILE0_PIECES = [(0, 256), (256, 512), (512, 768), (768, 896), (896, 1024)]
+TILE0_ON_VECTOR = (2, 4)
 
 
 def tile_picked_phpair_abs_p_kernel(
@@ -33,16 +38,16 @@ def tile_picked_phpair_abs_p_kernel(
         right_sb = keep.tile([P, V // 16], U16, name="right_sb")
 
         nc.sync.dma_start(offs_sb[:], offs)
-        xs_all = keep.tile([P, T], U8, name="xs_all", tag="xs_then_w2", align_bytes=64)
+        xs_all = keep.tile([P, T], U8, name="xs_all", align_bytes=64)
         nc.scalar.dma_start(
             xs_all[:].bitcast(I32), x_scales[0].bitcast(I32).unsqueeze(1).to_broadcast([16, 8, T // 4])
         )
         xw_all = keep.tile([P, T], U32, name="xw_all", align_bytes=64)
         nc.sync.dma_start(xw_all[:].bitcast(I32), x_words[0].rearrange("p n t -> p (n t)").bitcast(I32))
         w1_rows = w1.rearrange("(p j) c -> p j c", j=4)
-        w1_raw = [keep.tile([P, 2, H], F32, name="w1_raw%d" % a, align_bytes=64) for a in range(2)]
-        for a in range(2):
-            nc.sync.dma_start(w1_raw[a][:], w1_rows[:, 2 * a : 2 * a + 2, :])
+        w1_raw = [keep.tile([P, 2, H], F32, name="w1_raw%d" % half, align_bytes=64) for half in range(2)]
+        for half in range(2):
+            nc.sync.dma_start(w1_raw[half][:], w1_rows[:, 2 * half : 2 * half + 2, :])
         nc.sync.dma_start(left_sb[:], left)
         nc.sync.dma_start(right_sb[:], right)
 
@@ -60,16 +65,28 @@ def tile_picked_phpair_abs_p_kernel(
             queue.dma_start(xs[r:P:32, :].bitcast(I32), xs_picked[8 * r : P : 32, :].bitcast(I32))
 
         xw = keep.tile([P, S], U32, name="xw", align_bytes=64)
-        nc.vector.tensor_copy(xw[:], xw_all[:].indirect(offs_sb[:]))
+        for a in (0, BANK):
+            nc.vector.tensor_copy(xw[:, a : a + BANK], xw_all[:].indirect(offs_sb[:, a // 16 : (a + BANK) // 16]))
+        for bank in (6, 7):
+            idle = psum.tile([P, BANK], F32, name="idle", tag="bank%d" % bank)
+            nc.tensor.matmul_mx(
+                out=idle[:],
+                lhsT=xw[:, 0:P].bitcast(FP8X4),
+                lhsT_scale=xs_picked[:, 0:P],
+                rhs=xw[:, 0:BANK].bitcast(FP8X4),
+                rhs_scale=xs_picked[:, 0:BANK],
+                start=True,
+                stop=True,
+            )
 
-        w1_bf = [keep.tile([P, 2 * P * 4], BF16, name="w1_bf%d" % b, align_bytes=64) for b in range(2)]
+        w1_bf = [keep.tile([P, 2 * P * 4], BF16, name="w1_bf%d" % pair, align_bytes=64) for pair in range(2)]
 
-        def cast(copy, a, t0, t1):
+        def cast(copy, half, t0, t1):
             copy(
                 w1_bf[t0 // 2][:].rearrange("p (t m j) -> p m t j", t=2, j=4)[
-                    :, :, t0 % 2 : t0 % 2 + t1 - t0, 2 * a : 2 * a + 2
+                    :, :, t0 % 2 : t0 % 2 + t1 - t0, 2 * half : 2 * half + 2
                 ],
-                w1_raw[a][:].rearrange("p j (m t) -> p m t j", t=4)[:, :, t0:t1, :],
+                w1_raw[half][:].rearrange("p j (m t) -> p m t j", t=4)[:, :, t0:t1, :],
             )
 
         cast(nc.scalar.copy, 0, 0, 2)
@@ -87,7 +104,9 @@ def tile_picked_phpair_abs_p_kernel(
                 w2_scales[0, 4 * q : 4 * q + 4, :].bitcast(I32).unsqueeze(0).to_broadcast([8, 4, N // 4]),
             )
 
-        w1w = [keep.tile([P, P], U32, name="w1w%d" % t, align_bytes=64) for t in range(4)]
+        w1w = [
+            keep.tile([P, P], U32, name="w1w", tag="diff" if t == 2 else "w1w%d" % t, align_bytes=64) for t in range(4)
+        ]
         w1s = [keep.tile([P, P], U8, name="w1s%d" % t, align_bytes=64) for t in range(4)]
         h = [keep.tile([P, S], F32, name="h%d" % t) for t in range(4)]
 
@@ -113,19 +132,22 @@ def tile_picked_phpair_abs_p_kernel(
 
         quantize_w1(0)
         quantize_w1(1)
-        for u, (a, b) in enumerate([(0, 256), (256, 512), (512, 768), (768, 896), (896, 1024)]):
-            project(0, a, b, u, nc.vector.tensor_copy if u == 3 else nc.scalar.copy)
+        for bank, (a, b) in enumerate(TILE0_PIECES):
+            project(0, a, b, bank, nc.vector.tensor_copy if bank in TILE0_ON_VECTOR else nc.scalar.copy)
         quantize_w1(2)
         quantize_w1(3)
-        for t in range(1, 4):
-            for u in range(2):
-                project(t, BANK * u, BANK * (u + 1), (2 * t + 3 + u) % 8, nc.scalar.copy)
+        for u, bank in enumerate((5, 6, 7, 0)):
+            project(1, QUARTER * u, QUARTER * (u + 1), bank, nc.scalar.copy)
+        for a, b, bank in ((0, BANK, 1), (BANK, S - QUARTER, 2), (S - QUARTER, S, 0)):
+            project(2, a, b, bank, nc.scalar.copy)
+        for u in range(2):
+            project(3, BANK * u, BANK * (u + 1), 3 + u, nc.scalar.copy)
 
         z = [keep.tile([P, 4 * (b - a)], BF16, name="z%d" % c, align_bytes=64) for c, (a, b) in enumerate(CHUNKS)]
         out_rows = out.rearrange("(a p) v -> p a v", p=P)
 
-        def fetch_left(dst, t, a, b):
-            nc.vector.tensor_copy(dst, h[t][:].indirect(left_sb[:, a // 16 : b // 16]))
+        def fetch_left(dst, t):
+            nc.vector.tensor_copy(dst, h[t][:].indirect(left_sb[:]))
 
         def fetch_right(dst, t, a, b, picked):
             nc.vector.tensor_tensor(dst, h[t][:].indirect(right_sb[:, a // 16 : b // 16]), picked, SUB)
@@ -140,9 +162,6 @@ def tile_picked_phpair_abs_p_kernel(
         zw = [keep.tile([P, b - a], U32, name="zw%d" % a, align_bytes=64) for a, b in CHUNKS]
         zs = [keep.tile([P, b - a], U8, name="zs%d" % a, align_bytes=64) for a, b in CHUNKS]
 
-        def quantize_z(c):
-            nc.vector.quantize_mx(out=zw[c][:].bitcast(FP8X4), scales=zs[c][:], in_=z[c][:])
-
         def second_product(res, c, m):
             nc.tensor.matmul_mx(
                 out=res,
@@ -154,13 +173,13 @@ def tile_picked_phpair_abs_p_kernel(
                 stop=True,
             )
 
-        def finish(c, copy):
+        def finish_whole(c, bank):
             a, b = CHUNKS[c]
-            res = psum.tile([P, 2, b - a], F32, name="res", tag="bank%d" % (4 + c))
+            res = psum.tile([P, 2, b - a], F32, name="res", tag="bank%d" % bank)
             for m in range(2):
                 second_product(res[:, m, :], c, m)
             staged = keep.tile([P, 2, b - a], F32, name="staged%d" % c)
-            copy(staged[:], res[:])
+            nc.scalar.copy(staged[:], res[:])
             nc.sync.dma_start(out_rows[:, :, a:b], staged[:])
 
         def finish_split(c, bank, queues):
@@ -172,37 +191,26 @@ def tile_picked_phpair_abs_p_kernel(
                 copy(staged[:], res[:])
                 queues[m].dma_start(out_rows[:, m, a:b], staged[:])
 
-        half = V // 2
-        d01 = [keep.tile([P, 2, half], F32, name="d01", tag="pair%d" % u) for u in range(2)]
-        for t in range(2):
-            picked = [keep.tile([P, half], F32, name="left%d_%d" % (t, u)) for u in range(2)]
-            for u in range(2):
-                fetch_left(picked[u][:], t, half * u, half * (u + 1))
-            for u in range(2):
-                fetch_right(d01[u][:, t, :], t, half * u, half * (u + 1), picked[u][:])
+        lefts = [keep.tile([P, V], F32, name="left%d" % t) for t in range(4)]
+        d01 = keep.tile([P, 2, V], F32, name="d01", tag="diff", align_bytes=64)
+        for t in (0, 1):
+            fetch_left(lefts[t][:], t)
+        for t in (0, 1):
+            fetch_right(d01[:, t, :], t, 0, V, lefts[t][:])
         for c, (a, b) in enumerate(CHUNKS):
-            take_abs(c, 0, d01[a // half][:, :, a % half : a % half + b - a])
+            take_abs(c, 0, d01[:, :, a:b])
 
-        def fetch_left23(u, tag):
-            picked = keep.tile([P, 2, half], F32, name="left23", tag=tag)
+        for t in (2, 3):
+            fetch_left(lefts[t][:], t)
+        d23 = keep.tile([P, 2 * V], F32, name="d23", tag="diff", align_bytes=64)
+        for c, (a, b) in enumerate(CHUNKS):
+            rows = d23[:, 2 * a : 2 * b].rearrange("p (t v) -> p t v", t=2)
             for t in (2, 3):
-                fetch_left(picked[:, t - 2, :], t, half * u, half * (u + 1))
-            return picked
+                fetch_right(rows[:, t - 2, :], t, a, b, lefts[t][:, a:b])
+            take_abs(c, 1, rows)
 
-        def fetch_chunk(c, picked, tag):
-            a, b = CHUNKS[c]
-            d23 = keep.tile([P, 2, b - a], F32, name="d23", tag=tag)
-            for t in (2, 3):
-                fetch_right(d23[:, t - 2, :], t, a, b, picked[:, t - 2, a % half : a % half + b - a])
-            take_abs(c, 1, d23[:])
-
-        fetch_chunk(0, fetch_left23(0, "left23"), "pair0")
-        picked = fetch_left23(1, "pair1")
-        fetch_chunk(1, picked, "d23")
-        quantize_z(0)
-        fetch_chunk(2, picked, "pair0")
-        quantize_z(1)
-        quantize_z(2)
-        finish_split(0, 3, (nc.sync, nc.sync))
-        finish(1, nc.scalar.copy)
+        for c in range(len(CHUNKS)):
+            nc.vector.quantize_mx(out=zw[c][:].bitcast(FP8X4), scales=zs[c][:], in_=z[c][:])
+        finish_split(0, 1, (nc.sync, nc.sync))
+        finish_whole(1, 5)
         finish_split(2, 6, (nc.sync, nc.scalar))

@@ -22,7 +22,7 @@ QUARTER = S // 4
 CHUNKS = [(0, 256), (256, 384), (384, 512)]
 
 TILE0_PIECES = [(0, 256), (256, 512), (512, 768), (768, 896), (896, 1024)]
-TILE0_ON_VECTOR = (2, 4)
+TILE0_ON_VECTOR = (1, 3)
 
 
 def tile_picked_phpair_abs_p_kernel(
@@ -81,17 +81,21 @@ def tile_picked_phpair_abs_p_kernel(
 
         w1_bf = [keep.tile([P, 2 * P * 4], BF16, name="w1_bf%d" % pair, align_bytes=64) for pair in range(2)]
 
-        def cast(copy, half, t0, t1):
+        def pool_cast(dst, src):
+            nc.gpsimd.tensor_scalar(dst, src, 1.0, 0.0, mybir.AluOpType.mult, mybir.AluOpType.add)
+
+        def cast(copy, half, t0, t1, m0=0, m1=P):
             copy(
                 w1_bf[t0 // 2][:].rearrange("p (t m j) -> p m t j", t=2, j=4)[
-                    :, :, t0 % 2 : t0 % 2 + t1 - t0, 2 * half : 2 * half + 2
+                    :, m0:m1, t0 % 2 : t0 % 2 + t1 - t0, 2 * half : 2 * half + 2
                 ],
-                w1_raw[half][:].rearrange("p j (m t) -> p m t j", t=4)[:, :, t0:t1, :],
+                w1_raw[half][:].rearrange("p j (m t) -> p m t j", t=4)[:, m0:m1, t0:t1, :],
             )
 
         cast(nc.scalar.copy, 0, 0, 2)
-        cast(nc.scalar.copy, 0, 2, 4)
-        cast(nc.vector.tensor_copy, 1, 0, 1)
+        cast(pool_cast, 0, 2, 4)
+        cast(nc.scalar.copy, 1, 0, 1, 0, P // 2)
+        cast(nc.vector.tensor_copy, 1, 0, 1, P // 2, P)
         cast(nc.vector.tensor_copy, 1, 1, 2)
         cast(nc.scalar.copy, 1, 2, 4)
 

@@ -108,16 +108,18 @@ def tile_picked_phpair_abs_p_kernel(
                 w2_scales[0, 4 * q : 4 * q + 4, :].bitcast(I32).unsqueeze(0).to_broadcast([8, 4, N // 4]),
             )
 
-        w1w = [
-            keep.tile([P, P], U32, name="w1w", tag="diff" if t == 2 else "w1w%d" % t, align_bytes=64) for t in range(4)
-        ]
-        w1s = [keep.tile([P, P], U8, name="w1s%d" % t, align_bytes=64) for t in range(4)]
+        w1w_late = keep.tile([P, 2 * P], U32, name="w1w_late", tag="diff", align_bytes=64)
+        w1s_late = keep.tile([P, 2 * P], U8, name="w1s_late", align_bytes=64)
+        w1w = [keep.tile([P, P], U32, name="w1w%d" % t, align_bytes=64)[:] for t in range(2)]
+        w1s = [keep.tile([P, P], U8, name="w1s%d" % t, align_bytes=64)[:] for t in range(2)]
+        w1w = w1w + [w1w_late[:, 0:P], w1w_late[:, P : 2 * P]]
+        w1s = w1s + [w1s_late[:, 0:P], w1s_late[:, P : 2 * P]]
         h = [keep.tile([P, S], F32, name="h%d" % t) for t in range(4)]
 
         def quantize_w1(t):
             nc.vector.quantize_mx(
-                out=w1w[t][:].bitcast(FP8X4),
-                scales=w1s[t][:],
+                out=w1w[t].bitcast(FP8X4),
+                scales=w1s[t],
                 in_=w1_bf[t // 2][:, (t % 2) * 4 * P : (t % 2 + 1) * 4 * P],
             )
 
@@ -125,8 +127,8 @@ def tile_picked_phpair_abs_p_kernel(
             acc = psum.tile([P, b - a], F32, name="acc", tag="bank%d" % bank)
             nc.tensor.matmul_mx(
                 out=acc[:],
-                lhsT=w1w[t][:].bitcast(FP8X4),
-                lhsT_scale=w1s[t][:],
+                lhsT=w1w[t].bitcast(FP8X4),
+                lhsT_scale=w1s[t],
                 rhs=xw[:, a:b].bitcast(FP8X4),
                 rhs_scale=xs[:, a:b],
                 start=True,
@@ -138,8 +140,7 @@ def tile_picked_phpair_abs_p_kernel(
         quantize_w1(1)
         for bank, (a, b) in enumerate(TILE0_PIECES):
             project(0, a, b, bank, nc.vector.tensor_copy if bank in TILE0_ON_VECTOR else nc.scalar.copy)
-        quantize_w1(2)
-        quantize_w1(3)
+        nc.vector.quantize_mx(out=w1w_late[:].bitcast(FP8X4), scales=w1s_late[:], in_=w1_bf[1][:])
         for u, bank in enumerate((5, 6, 7, 0)):
             project(1, QUARTER * u, QUARTER * (u + 1), bank, nc.scalar.copy)
         for a, b, bank in ((0, BANK, 1), (BANK, S - QUARTER, 2), (S - QUARTER, S, 0)):
@@ -216,5 +217,11 @@ def tile_picked_phpair_abs_p_kernel(
         for c in range(len(CHUNKS)):
             nc.vector.quantize_mx(out=zw[c][:].bitcast(FP8X4), scales=zs[c][:], in_=z[c][:])
         finish_split(0, 1, (nc.sync, nc.sync))
-        finish_whole(1, 5)
-        finish_split(2, 6, (nc.sync, nc.scalar))
+        late = [keep.tile([P, 2 * P], F32, name="late%d" % m) for m in range(2)]
+        for c, banks in ((1, (3, 4)), (2, (6, 7))):
+            for m, copy in enumerate((nc.vector.tensor_copy, nc.scalar.copy)):
+                res = psum.tile([P, P], F32, name="res", tag="bank%d" % banks[m])
+                second_product(res[:], c, m)
+                copy(late[m][:, (c - 1) * P : c * P], res[:])
+        for m, queue in enumerate((nc.sync, nc.scalar)):
+            queue.dma_start(out_rows[:, m, 2 * P : V], late[m][:])

@@ -14,6 +14,8 @@ U8 = mybir.dt.uint8
 FP8X4 = mybir.dt.float8_e4m3fn_x4
 ABS = mybir.ActivationFunctionType.Abs
 SUB = mybir.AluOpType.subtract
+MULT = mybir.AluOpType.mult
+ADD = mybir.AluOpType.add
 
 P = 128
 BANK = 512
@@ -61,8 +63,7 @@ def tile_picked_phpair_abs_p_kernel(
         xs_picked = keep.tile([P, S], U8, name="xs_picked", align_bytes=64)
         nc.vector.tensor_copy(xs_picked[:], xs_all[:].indirect(offs_sb[:]))
         for r in range(4):
-            queue = nc.sync if r % 2 else nc.scalar
-            queue.dma_start(xs[r:P:32, :].bitcast(I32), xs_picked[8 * r : P : 32, :].bitcast(I32))
+            nc.scalar.dma_start(xs[r:P:32, :].bitcast(I32), xs_picked[8 * r : P : 32, :].bitcast(I32))
 
         xw = keep.tile([P, S], U32, name="xw", align_bytes=64)
         for a in (0, BANK):
@@ -81,8 +82,8 @@ def tile_picked_phpair_abs_p_kernel(
 
         w1_bf = [keep.tile([P, 2 * P * 4], BF16, name="w1_bf%d" % pair, align_bytes=64) for pair in range(2)]
 
-        def pool_cast(dst, src):
-            nc.gpsimd.tensor_scalar(dst, src, 1.0, 0.0, mybir.AluOpType.mult, mybir.AluOpType.add)
+        def gpsimd_copy(dst, src):
+            nc.gpsimd.tensor_scalar(dst, src, 1.0, 0.0, MULT, ADD)
 
         def cast(copy, half, t0, t1, m0=0, m1=P):
             copy(
@@ -93,7 +94,7 @@ def tile_picked_phpair_abs_p_kernel(
             )
 
         cast(nc.scalar.copy, 0, 0, 2)
-        cast(pool_cast, 0, 2, 4)
+        cast(gpsimd_copy, 0, 2, 4)
         cast(nc.scalar.copy, 1, 0, 1, 0, P // 2)
         cast(nc.vector.tensor_copy, 1, 0, 1, P // 2, P)
         cast(nc.vector.tensor_copy, 1, 1, 2)
@@ -116,13 +117,6 @@ def tile_picked_phpair_abs_p_kernel(
         w1s = w1s + [w1s_late[:, 0:P], w1s_late[:, P : 2 * P]]
         h = [keep.tile([P, S], F32, name="h%d" % t) for t in range(4)]
 
-        def quantize_w1(t):
-            nc.vector.quantize_mx(
-                out=w1w[t].bitcast(FP8X4),
-                scales=w1s[t],
-                in_=w1_bf[t // 2][:, (t % 2) * 4 * P : (t % 2 + 1) * 4 * P],
-            )
-
         def project(t, a, b, bank, copy):
             acc = psum.tile([P, b - a], F32, name="acc", tag="bank%d" % bank)
             nc.tensor.matmul_mx(
@@ -136,8 +130,10 @@ def tile_picked_phpair_abs_p_kernel(
             )
             copy(h[t][:, a:b], acc[:])
 
-        quantize_w1(0)
-        quantize_w1(1)
+        for t in range(2):
+            nc.vector.quantize_mx(
+                out=w1w[t].bitcast(FP8X4), scales=w1s[t], in_=w1_bf[0][:, t * 4 * P : (t + 1) * 4 * P]
+            )
         for bank, (a, b) in enumerate(TILE0_PIECES):
             project(0, a, b, bank, nc.vector.tensor_copy if bank in TILE0_ON_VECTOR else nc.scalar.copy)
         nc.vector.quantize_mx(out=w1w_late[:].bitcast(FP8X4), scales=w1s_late[:], in_=w1_bf[1][:])
@@ -168,33 +164,16 @@ def tile_picked_phpair_abs_p_kernel(
         zs = [keep.tile([P, b - a], U8, name="zs%d" % a, align_bytes=64) for a, b in CHUNKS]
 
         def second_product(res, c, m):
-            nc.tensor.matmul_mx(
-                out=res,
-                lhsT=w2w[:, m * P : (m + 1) * P].bitcast(FP8X4),
-                lhsT_scale=w2s[:, m * P : (m + 1) * P],
-                rhs=zw[c][:].bitcast(FP8X4),
-                rhs_scale=zs[c][:],
-                start=True,
-                stop=True,
-            )
-
-        def finish_whole(c, bank):
-            a, b = CHUNKS[c]
-            res = psum.tile([P, 2, b - a], F32, name="res", tag="bank%d" % bank)
-            for m in range(2):
-                second_product(res[:, m, :], c, m)
-            staged = keep.tile([P, 2, b - a], F32, name="staged%d" % c)
-            nc.scalar.copy(staged[:], res[:])
-            nc.sync.dma_start(out_rows[:, :, a:b], staged[:])
-
-        def finish_split(c, bank, queues):
-            a, b = CHUNKS[c]
-            for m, copy in enumerate((nc.vector.tensor_copy, nc.scalar.copy)):
-                res = psum.tile([P, b - a], F32, name="res", tag="bank%d" % (bank + m))
-                second_product(res[:], c, m)
-                staged = keep.tile([P, b - a], F32, name="last%d_%d" % (c, m))
-                copy(staged[:], res[:])
-                queues[m].dma_start(out_rows[:, m, a:b], staged[:])
+            for u in range(0, CHUNKS[c][1] - CHUNKS[c][0], P):
+                nc.tensor.matmul_mx(
+                    out=res[:, u : u + P],
+                    lhsT=w2w[:, m * P : (m + 1) * P].bitcast(FP8X4),
+                    lhsT_scale=w2s[:, m * P : (m + 1) * P],
+                    rhs=zw[c][:, u : u + P].bitcast(FP8X4),
+                    rhs_scale=zs[c][:, u : u + P],
+                    start=True,
+                    stop=True,
+                )
 
         lefts = [keep.tile([P, V], F32, name="left%d" % t) for t in range(4)]
         d01 = keep.tile([P, 2, V], F32, name="d01", tag="diff", align_bytes=64)
@@ -214,14 +193,26 @@ def tile_picked_phpair_abs_p_kernel(
                 fetch_right(rows[:, t - 2, :], t, a, b, lefts[t][:, a:b])
             take_abs(c, 1, rows)
 
-        for c in range(len(CHUNKS)):
-            nc.vector.quantize_mx(out=zw[c][:].bitcast(FP8X4), scales=zs[c][:], in_=z[c][:])
-        finish_split(0, 1, (nc.sync, nc.sync))
-        late = [keep.tile([P, 2 * P], F32, name="late%d" % m) for m in range(2)]
+        for c, (a, b) in enumerate(CHUNKS):
+            for u in range(0, b - a, P):
+                nc.vector.quantize_mx(
+                    out=zw[c][:, u : u + P].bitcast(FP8X4), scales=zs[c][:, u : u + P], in_=z[c][:, 4 * u : 4 * (u + P)]
+                )
+
+        copies = (nc.scalar.copy, nc.vector.tensor_copy)
+        half_pairs = V // 2
+        for m, copy in enumerate(copies):
+            res = psum.tile([P, half_pairs], F32, name="res", tag="bank%d" % (1 + m))
+            second_product(res[:], 0, m)
+            early = keep.tile([P, half_pairs], F32, name="early%d" % m)
+            copy(early[:], res[:])
+            nc.sync.dma_start(out_rows[:, m, 0:half_pairs], early[:])
+        late = [keep.tile([P, half_pairs], F32, name="late%d" % m) for m in range(2)]
         for c, banks in ((1, (3, 4)), (2, (6, 7))):
-            for m, copy in enumerate((nc.vector.tensor_copy, nc.scalar.copy)):
-                res = psum.tile([P, P], F32, name="res", tag="bank%d" % banks[m])
+            a, b = CHUNKS[c]
+            for m, copy in enumerate(copies):
+                res = psum.tile([P, b - a], F32, name="res", tag="bank%d" % banks[m])
                 second_product(res[:], c, m)
-                copy(late[m][:, (c - 1) * P : c * P], res[:])
-        for m, queue in enumerate((nc.sync, nc.scalar)):
-            queue.dma_start(out_rows[:, m, 2 * P : V], late[m][:])
+                copy(late[m][:, a - half_pairs : b - half_pairs], res[:])
+        for m, queue in enumerate((nc.scalar, nc.sync)):
+            queue.dma_start(out_rows[:, m, half_pairs:V], late[m][:])

@@ -186,12 +186,16 @@ def tile_picked_phpair_abs_p_kernel(
 
         for t in (2, 3):
             fetch_left(lefts[t][:], t)
-        d23 = keep.tile([P, 2 * V], F32, name="d23", tag="diff", align_bytes=64)
-        for c, (a, b) in enumerate(CHUNKS):
-            rows = d23[:, 2 * a : 2 * b].rearrange("p (t v) -> p t v", t=2)
-            for t in (2, 3):
-                fetch_right(rows[:, t - 2, :], t, a, b, lefts[t][:, a:b])
-            take_abs(c, 1, rows)
+        half_pairs = V // 2
+        d23 = keep.tile([P, 2, 2, half_pairs], F32, name="d23", tag="diff", align_bytes=64)
+        for t in (2, 3):
+            fetch_right(d23[:, 0, t - 2, :], t, 0, half_pairs, lefts[t][:, 0:half_pairs])
+        take_abs(0, 1, d23[:, 0, :, :])
+        fetch_right(d23[:, 1, 0, :], 2, half_pairs, V, lefts[2][:, half_pairs:V])
+        for c in (1, 2):
+            a, b = CHUNKS[c]
+            fetch_right(d23[:, 1, 1, a - half_pairs : b - half_pairs], 3, a, b, lefts[3][:, a:b])
+            take_abs(c, 1, d23[:, 1, :, a - half_pairs : b - half_pairs])
 
         for c, (a, b) in enumerate(CHUNKS):
             for u in range(0, b - a, P):
@@ -200,7 +204,6 @@ def tile_picked_phpair_abs_p_kernel(
                 )
 
         copies = (nc.scalar.copy, nc.vector.tensor_copy)
-        half_pairs = V // 2
         for m, copy in enumerate(copies):
             res = psum.tile([P, half_pairs], F32, name="res", tag="bank%d" % (1 + m))
             second_product(res[:], 0, m)

@@ -13,13 +13,13 @@ U16 = mybir.dt.uint16
 U8 = mybir.dt.uint8
 FP8X4 = mybir.dt.float8_e4m3fn_x4
 ABS = mybir.ActivationFunctionType.Abs
+COPY = mybir.ActivationFunctionType.Copy
 SUB = mybir.AluOpType.subtract
 MULT = mybir.AluOpType.mult
 ADD = mybir.AluOpType.add
 
 P = 128
 BANK = 512
-QUARTER = S // 4
 
 CHUNKS = [(0, 256), (256, 384), (384, 512)]
 
@@ -66,19 +66,7 @@ def tile_picked_phpair_abs_p_kernel(
             nc.scalar.dma_start(xs[r:P:32, :].bitcast(I32), xs_picked[8 * r : P : 32, :].bitcast(I32))
 
         xw = keep.tile([P, S], U32, name="xw", align_bytes=64)
-        for a in (0, BANK):
-            nc.vector.tensor_copy(xw[:, a : a + BANK], xw_all[:].indirect(offs_sb[:, a // 16 : (a + BANK) // 16]))
-        for bank in (6, 7):
-            idle = psum.tile([P, BANK], F32, name="idle", tag="bank%d" % bank)
-            nc.tensor.matmul_mx(
-                out=idle[:],
-                lhsT=xw[:, 0:P].bitcast(FP8X4),
-                lhsT_scale=xs_picked[:, 0:P],
-                rhs=xw[:, 0:BANK].bitcast(FP8X4),
-                rhs_scale=xs_picked[:, 0:BANK],
-                start=True,
-                stop=True,
-            )
+        nc.vector.tensor_copy(xw[:], xw_all[:].indirect(offs_sb[:]))
 
         w1_bf = [keep.tile([P, 2 * P * 4], BF16, name="w1_bf%d" % pair, align_bytes=64) for pair in range(2)]
 
@@ -109,7 +97,7 @@ def tile_picked_phpair_abs_p_kernel(
                 w2_scales[0, 4 * q : 4 * q + 4, :].bitcast(I32).unsqueeze(0).to_broadcast([8, 4, N // 4]),
             )
 
-        w1w_late = keep.tile([P, 2 * P], U32, name="w1w_late", tag="diff", align_bytes=64)
+        w1w_late = keep.tile([P, 2 * P], U32, name="w1w_late", align_bytes=64)
         w1s_late = keep.tile([P, 2 * P], U8, name="w1s_late", align_bytes=64)
         w1w = [keep.tile([P, P], U32, name="w1w%d" % t, align_bytes=64)[:] for t in range(2)]
         w1s = [keep.tile([P, P], U8, name="w1s%d" % t, align_bytes=64)[:] for t in range(2)]
@@ -137,25 +125,23 @@ def tile_picked_phpair_abs_p_kernel(
         for bank, (a, b) in enumerate(TILE0_PIECES):
             project(0, a, b, bank, nc.vector.tensor_copy if bank in TILE0_ON_VECTOR else nc.scalar.copy)
         nc.vector.quantize_mx(out=w1w_late[:].bitcast(FP8X4), scales=w1s_late[:], in_=w1_bf[1][:])
-        for u, bank in enumerate((5, 6, 7, 0)):
-            project(1, QUARTER * u, QUARTER * (u + 1), bank, nc.scalar.copy)
-        for a, b, bank in ((0, BANK, 1), (BANK, S - QUARTER, 2), (S - QUARTER, S, 0)):
-            project(2, a, b, bank, nc.scalar.copy)
         for u in range(2):
-            project(3, BANK * u, BANK * (u + 1), 3 + u, nc.scalar.copy)
+            project(1, BANK * u, BANK * (u + 1), 5 + u, nc.vector.tensor_copy)
+        for u, bank in enumerate((7, 0)):
+            project(2, BANK * u, BANK * (u + 1), bank, nc.vector.tensor_copy)
 
-        z = [keep.tile([P, 4 * (b - a)], BF16, name="z%d" % c, align_bytes=64) for c, (a, b) in enumerate(CHUNKS)]
+        z = keep.tile([P, 4 * V], BF16, name="z", align_bytes=64)
         out_rows = out.rearrange("(a p) v -> p a v", p=P)
 
         def fetch_left(dst, t):
-            nc.vector.tensor_copy(dst, h[t][:].indirect(left_sb[:]))
+            nc.scalar.activation(dst, h[t][:].indirect(left_sb[:]), COPY)
 
         def fetch_right(dst, t, a, b, picked):
             nc.vector.tensor_tensor(dst, h[t][:].indirect(right_sb[:, a // 16 : b // 16]), picked, SUB)
 
-        def take_abs(c, pair, src):
+        def take_abs(a, b, pair, src):
             nc.scalar.activation(
-                z[c][:].rearrange("p (v t) -> p v t", t=4)[:, :, 2 * pair : 2 * pair + 2],
+                z[:].rearrange("p (v t) -> p v t", t=4)[:, a:b, 2 * pair : 2 * pair + 2],
                 src.rearrange("p t v -> p v t"),
                 ABS,
             )
@@ -175,32 +161,28 @@ def tile_picked_phpair_abs_p_kernel(
                     stop=True,
                 )
 
-        lefts = [keep.tile([P, V], F32, name="left%d" % t) for t in range(4)]
-        d01 = keep.tile([P, 2, V], F32, name="d01", tag="diff", align_bytes=64)
-        for t in (0, 1):
-            fetch_left(lefts[t][:], t)
-        for t in (0, 1):
-            fetch_right(d01[:, t, :], t, 0, V, lefts[t][:])
-        for c, (a, b) in enumerate(CHUNKS):
-            take_abs(c, 0, d01[:, :, a:b])
-
-        for t in (2, 3):
-            fetch_left(lefts[t][:], t)
         half_pairs = V // 2
-        d23 = keep.tile([P, 2, 2, half_pairs], F32, name="d23", tag="diff", align_bytes=64)
+        lefts = [keep.tile([P, V], F32, name="left%d" % t) for t in range(4)]
+        d01 = keep.tile([P, 2, V], F32, name="d01", align_bytes=64)
+        d23 = keep.tile([P, 2, V], F32, name="d23", align_bytes=64)
+        for t in (0, 1):
+            fetch_left(lefts[t][:], t)
+        fetch_right(d01[:, 0, :], 0, 0, V, lefts[0][:])
+        project(3, 0, BANK, 6, nc.scalar.copy)
+        project(3, BANK, S, 5, nc.vector.tensor_copy)
         for t in (2, 3):
-            fetch_right(d23[:, 0, t - 2, :], t, 0, half_pairs, lefts[t][:, 0:half_pairs])
-        take_abs(0, 1, d23[:, 0, :, :])
-        fetch_right(d23[:, 1, 0, :], 2, half_pairs, V, lefts[2][:, half_pairs:V])
-        for c in (1, 2):
-            a, b = CHUNKS[c]
-            fetch_right(d23[:, 1, 1, a - half_pairs : b - half_pairs], 3, a, b, lefts[3][:, a:b])
-            take_abs(c, 1, d23[:, 1, :, a - half_pairs : b - half_pairs])
+            fetch_left(lefts[t][:], t)
+        fetch_right(d01[:, 1, :], 1, 0, V, lefts[1][:])
+        take_abs(0, V, 0, d01[:])
+        fetch_right(d23[:, 0, :], 2, 0, V, lefts[2][:])
+        for a, b in CHUNKS:
+            fetch_right(d23[:, 1, a:b], 3, a, b, lefts[3][:, a:b])
+            take_abs(a, b, 1, d23[:, :, a:b])
 
         for c, (a, b) in enumerate(CHUNKS):
             for u in range(0, b - a, P):
                 nc.vector.quantize_mx(
-                    out=zw[c][:, u : u + P].bitcast(FP8X4), scales=zs[c][:, u : u + P], in_=z[c][:, 4 * u : 4 * (u + P)]
+                    out=zw[c][:, u : u + P].bitcast(FP8X4), scales=zs[c][:, u : u + P], in_=z[:, 4 * (a + u) : 4 * (a + u + P)]
                 )
 
         copies = (nc.scalar.copy, nc.vector.tensor_copy)

@@ -16,10 +16,12 @@ ABS = mybir.ActivationFunctionType.Abs
 COPY = mybir.ActivationFunctionType.Copy
 SUB = mybir.AluOpType.subtract
 MULT = mybir.AluOpType.mult
-ADD = mybir.AluOpType.add
+MAX = mybir.AluOpType.max
 
 P = 128
 BANK = 512
+QUARTER = S // 4
+ON_VECTOR = 96
 
 CHUNKS = [(0, 256), (256, 384), (384, 512)]
 
@@ -47,9 +49,9 @@ def tile_picked_phpair_abs_p_kernel(
         xw_all = keep.tile([P, T], U32, name="xw_all", align_bytes=64)
         nc.sync.dma_start(xw_all[:].bitcast(I32), x_words[0].rearrange("p n t -> p (n t)").bitcast(I32))
         w1_rows = w1.rearrange("(p j) c -> p j c", j=4)
-        w1_raw = [keep.tile([P, 2, H], F32, name="w1_raw%d" % half, align_bytes=64) for half in range(2)]
+        w1_raw = keep.tile([P, 4, H], F32, name="w1_raw", align_bytes=64)
         for half in range(2):
-            nc.sync.dma_start(w1_raw[half][:], w1_rows[:, 2 * half : 2 * half + 2, :])
+            nc.sync.dma_start(w1_raw[:, 2 * half : 2 * half + 2, :], w1_rows[:, 2 * half : 2 * half + 2, :])
         nc.sync.dma_start(left_sb[:], left)
         nc.sync.dma_start(right_sb[:], right)
 
@@ -58,7 +60,7 @@ def tile_picked_phpair_abs_p_kernel(
         nc.scalar.activation(warm[:, 1:2], warm[:, 0:1], ABS)
 
         xs = keep.tile([P, S], U8, name="xs", align_bytes=64)
-        nc.gpsimd.memset(xs[:].bitcast(I32), 0)
+        nc.vector.memset(xs[:].bitcast(I32), 0)
 
         xs_picked = keep.tile([P, S], U8, name="xs_picked", align_bytes=64)
         nc.vector.tensor_copy(xs_picked[:], xs_all[:].indirect(offs_sb[:]))
@@ -70,25 +72,19 @@ def tile_picked_phpair_abs_p_kernel(
 
         w1_bf = [keep.tile([P, 2 * P * 4], BF16, name="w1_bf%d" % pair, align_bytes=64) for pair in range(2)]
 
-        def gpsimd_copy(dst, src):
-            nc.gpsimd.tensor_scalar(dst, src, 1.0, 0.0, MULT, ADD)
-
-        def cast(copy, half, t0, t1, m0=0, m1=P):
+        def cast(copy, j0, j1, t0, t1, m0=0, m1=P):
             copy(
-                w1_bf[t0 // 2][:].rearrange("p (t m j) -> p m t j", t=2, j=4)[
-                    :, m0:m1, t0 % 2 : t0 % 2 + t1 - t0, 2 * half : 2 * half + 2
-                ],
-                w1_raw[half][:].rearrange("p j (m t) -> p m t j", t=4)[:, m0:m1, t0:t1, :],
+                w1_bf[t0 // 2][:].rearrange("p (t m j) -> p m t j", t=2, j=4)[:, m0:m1, t0 % 2 : t0 % 2 + t1 - t0, j0:j1],
+                w1_raw[:].rearrange("p j (m t) -> p m t j", t=4)[:, m0:m1, t0:t1, j0:j1],
             )
 
-        cast(nc.scalar.copy, 0, 0, 2)
-        cast(gpsimd_copy, 0, 2, 4)
-        cast(nc.scalar.copy, 1, 0, 1, 0, P // 2)
-        cast(nc.vector.tensor_copy, 1, 0, 1, P // 2, P)
-        cast(nc.vector.tensor_copy, 1, 1, 2)
-        cast(nc.scalar.copy, 1, 2, 4)
+        cast(nc.scalar.copy, 0, 2, 0, 2)
+        cast(nc.scalar.copy, 2, 4, 0, 1, 0, P // 2)
+        cast(nc.vector.tensor_copy, 2, 4, 0, 1, P // 2, P)
+        cast(nc.vector.tensor_copy, 2, 4, 1, 2)
+        cast(nc.scalar.copy, 0, 4, 2, 4)
 
-        w2w = keep.tile([P, N], U32, name="w2w", tag="w1_raw0", align_bytes=64)
+        w2w = keep.tile([P, N], U32, name="w2w", tag="w1_raw", align_bytes=64)
         nc.sync.dma_start(w2w[:].bitcast(I32), w2_words[0].rearrange("p n t -> p (n t)").bitcast(I32))
         w2s = keep.tile([P, N], U8, name="w2s", tag="xs_picked", align_bytes=64)
         for q in range(4):
@@ -125,25 +121,25 @@ def tile_picked_phpair_abs_p_kernel(
         for bank, (a, b) in enumerate(TILE0_PIECES):
             project(0, a, b, bank, nc.vector.tensor_copy if bank in TILE0_ON_VECTOR else nc.scalar.copy)
         nc.vector.quantize_mx(out=w1w_late[:].bitcast(FP8X4), scales=w1s_late[:], in_=w1_bf[1][:])
-        for u in range(2):
-            project(1, BANK * u, BANK * (u + 1), 5 + u, nc.vector.tensor_copy)
-        for u, bank in enumerate((7, 0)):
-            project(2, BANK * u, BANK * (u + 1), bank, nc.vector.tensor_copy)
+        for u, bank in enumerate((5, 6, 7, 0)):
+            project(1, QUARTER * u, QUARTER * (u + 1), bank, nc.vector.tensor_copy)
+        project(2, 0, BANK, 1, nc.scalar.copy)
+        project(2, BANK, S, 2, nc.vector.tensor_copy)
 
         z = keep.tile([P, 4 * V], BF16, name="z", align_bytes=64)
         out_rows = out.rearrange("(a p) v -> p a v", p=P)
 
-        def fetch_left(dst, t):
-            nc.scalar.activation(dst, h[t][:].indirect(left_sb[:]), COPY)
+        def fetch_left(t, a, b):
+            nc.scalar.activation(lefts[t][:, a:b], h[t][:].indirect(left_sb[:, a // 16 : b // 16]), COPY)
 
-        def fetch_right(dst, t, a, b, picked):
-            nc.vector.tensor_tensor(dst, h[t][:].indirect(right_sb[:, a // 16 : b // 16]), picked, SUB)
+        def fetch_right(t, a, b):
+            nc.vector.tensor_tensor(
+                diff[:, t, a:b], h[t][:].indirect(right_sb[:, a // 16 : b // 16]), lefts[t][:, a:b], SUB
+            )
 
-        def take_abs(a, b, pair, src):
+        def take_abs(a, b):
             nc.scalar.activation(
-                z[:].rearrange("p (v t) -> p v t", t=4)[:, a:b, 2 * pair : 2 * pair + 2],
-                src.rearrange("p t v -> p v t"),
-                ABS,
+                z[:, 4 * a : 4 * b].rearrange("p (v t) -> p v t", t=4), diff[:, :, a:b].rearrange("p t v -> p v t"), ABS
             )
 
         zw = [keep.tile([P, b - a], U32, name="zw%d" % a, align_bytes=64) for a, b in CHUNKS]
@@ -163,21 +159,25 @@ def tile_picked_phpair_abs_p_kernel(
 
         half_pairs = V // 2
         lefts = [keep.tile([P, V], F32, name="left%d" % t) for t in range(4)]
-        d01 = keep.tile([P, 2, V], F32, name="d01", align_bytes=64)
-        d23 = keep.tile([P, 2, V], F32, name="d23", align_bytes=64)
+        diff = keep.tile([P, 4, V], F32, name="diff", align_bytes=64)
         for t in (0, 1):
-            fetch_left(lefts[t][:], t)
-        fetch_right(d01[:, 0, :], 0, 0, V, lefts[0][:])
-        project(3, 0, BANK, 6, nc.scalar.copy)
-        project(3, BANK, S, 5, nc.vector.tensor_copy)
-        for t in (2, 3):
-            fetch_left(lefts[t][:], t)
-        fetch_right(d01[:, 1, :], 1, 0, V, lefts[1][:])
-        take_abs(0, V, 0, d01[:])
-        fetch_right(d23[:, 0, :], 2, 0, V, lefts[2][:])
+            fetch_left(t, 0, V)
+        project(3, 0, BANK, 3, nc.scalar.copy)
+        project(3, BANK, S, 4, nc.vector.tensor_copy)
+        fetch_right(0, 0, V)
+        for a in (0, half_pairs):
+            for t in (2, 3):
+                fetch_left(t, a, a + half_pairs)
         for a, b in CHUNKS:
-            fetch_right(d23[:, 1, a:b], 3, a, b, lefts[3][:, a:b])
-            take_abs(a, b, 1, d23[:, :, a:b])
+            if a % half_pairs == 0:
+                for t in (1, 2):
+                    fetch_right(t, a, a + half_pairs)
+            fetch_right(3, a, b)
+            take_abs(a, min(b, V - ON_VECTOR))
+        last = diff[:, :, V - ON_VECTOR : V].rearrange("p t v -> p v t")
+        nc.vector.scalar_tensor_tensor(
+            z[:, 4 * (V - ON_VECTOR) : 4 * V].rearrange("p (v t) -> p v t", t=4), last, -1.0, last, MULT, MAX
+        )
 
         for c, (a, b) in enumerate(CHUNKS):
             for u in range(0, b - a, P):

@@ -21,7 +21,7 @@ MAX = mybir.AluOpType.max
 P = 128
 BANK = 512
 QUARTER = S // 4
-ON_VECTOR = 96
+ON_VECTOR = 64
 
 CHUNKS = [(0, 256), (256, 384), (384, 512)]
 
@@ -67,22 +67,23 @@ def tile_picked_phpair_abs_p_kernel(
         for r in range(4):
             nc.scalar.dma_start(xs[r:P:32, :].bitcast(I32), xs_picked[8 * r : P : 32, :].bitcast(I32))
 
-        xw = keep.tile([P, S], U32, name="xw", align_bytes=64)
-        nc.vector.tensor_copy(xw[:], xw_all[:].indirect(offs_sb[:]))
+        xw = keep.tile([P, S - QUARTER], U32, name="xw", align_bytes=64)
+        nc.vector.tensor_copy(xw[:], xw_all[:].indirect(offs_sb[:, 0 : (S - QUARTER) // 16]))
 
-        w1_bf = [keep.tile([P, 2 * P * 4], BF16, name="w1_bf%d" % pair, align_bytes=64) for pair in range(2)]
+        w1_bf = [keep.tile([P, n * P * 4], BF16, name="w1_bf%d" % u, align_bytes=64) for u, n in enumerate((1, 1, 2))]
 
-        def cast(copy, j0, j1, t0, t1, m0=0, m1=P):
+        def cast(copy, u, t0, t1, j0, j1, m0=0, m1=P):
             copy(
-                w1_bf[t0 // 2][:].rearrange("p (t m j) -> p m t j", t=2, j=4)[:, m0:m1, t0 % 2 : t0 % 2 + t1 - t0, j0:j1],
+                w1_bf[u][:].rearrange("p (t m j) -> p m t j", t=t1 - t0, j=4)[:, m0:m1, :, j0:j1],
                 w1_raw[:].rearrange("p j (m t) -> p m t j", t=4)[:, m0:m1, t0:t1, j0:j1],
             )
 
-        cast(nc.scalar.copy, 0, 2, 0, 2)
-        cast(nc.scalar.copy, 2, 4, 0, 1, 0, P // 2)
-        cast(nc.vector.tensor_copy, 2, 4, 0, 1, P // 2, P)
-        cast(nc.vector.tensor_copy, 2, 4, 1, 2)
-        cast(nc.scalar.copy, 0, 4, 2, 4)
+        for t in (0, 1):
+            cast(nc.scalar.copy, t, t, t + 1, 0, 2)
+        cast(nc.scalar.copy, 0, 0, 1, 2, 4, 0, P // 2)
+        cast(nc.vector.tensor_copy, 0, 0, 1, 2, 4, P // 2, P)
+        cast(nc.vector.tensor_copy, 1, 1, 2, 2, 4)
+        cast(nc.scalar.copy, 2, 2, 4, 0, 4)
 
         w2w = keep.tile([P, N], U32, name="w2w", tag="w1_raw", align_bytes=64)
         nc.sync.dma_start(w2w[:].bitcast(I32), w2_words[0].rearrange("p n t -> p (n t)").bitcast(I32))
@@ -101,32 +102,40 @@ def tile_picked_phpair_abs_p_kernel(
         w1s = w1s + [w1s_late[:, 0:P], w1s_late[:, P : 2 * P]]
         h = [keep.tile([P, S], F32, name="h%d" % t) for t in range(4)]
 
+        xw_last = keep.tile([P, QUARTER], U32, name="xw_last", tag="w1_bf0", align_bytes=64)
+
         def project(t, a, b, bank, copy):
             acc = psum.tile([P, b - a], F32, name="acc", tag="bank%d" % bank)
-            nc.tensor.matmul_mx(
-                out=acc[:],
-                lhsT=w1w[t].bitcast(FP8X4),
-                lhsT_scale=w1s[t],
-                rhs=xw[:, a:b].bitcast(FP8X4),
-                rhs_scale=xs[:, a:b],
-                start=True,
-                stop=True,
-            )
+            edge = S - QUARTER
+            for c, d in ((a, min(b, edge)), (max(a, edge), b)):
+                if c < d:
+                    nc.tensor.matmul_mx(
+                        out=acc[:, c - a : d - a],
+                        lhsT=w1w[t].bitcast(FP8X4),
+                        lhsT_scale=w1s[t],
+                        rhs=(xw[:, c:d] if c < edge else xw_last[:, c - edge : d - edge]).bitcast(FP8X4),
+                        rhs_scale=xs[:, c:d],
+                        start=True,
+                        stop=True,
+                    )
             copy(h[t][:, a:b], acc[:])
 
-        for t in range(2):
-            nc.vector.quantize_mx(
-                out=w1w[t].bitcast(FP8X4), scales=w1s[t], in_=w1_bf[0][:, t * 4 * P : (t + 1) * 4 * P]
-            )
+        nc.vector.quantize_mx(out=w1w[0].bitcast(FP8X4), scales=w1s[0], in_=w1_bf[0][:])
+        nc.vector.tensor_copy(xw_last[:], xw_all[:].indirect(offs_sb[:, (S - QUARTER) // 16 : S // 16]))
+        nc.vector.quantize_mx(out=w1w[1].bitcast(FP8X4), scales=w1s[1], in_=w1_bf[1][:])
         for bank, (a, b) in enumerate(TILE0_PIECES):
             project(0, a, b, bank, nc.vector.tensor_copy if bank in TILE0_ON_VECTOR else nc.scalar.copy)
-        nc.vector.quantize_mx(out=w1w_late[:].bitcast(FP8X4), scales=w1s_late[:], in_=w1_bf[1][:])
+        nc.vector.quantize_mx(out=w1w_late[:].bitcast(FP8X4), scales=w1s_late[:], in_=w1_bf[2][:])
         for u, bank in enumerate((5, 6, 7, 0)):
             project(1, QUARTER * u, QUARTER * (u + 1), bank, nc.vector.tensor_copy)
-        project(2, 0, BANK, 1, nc.scalar.copy)
         project(2, BANK, S, 2, nc.vector.tensor_copy)
+        project(2, 0, BANK, 1, nc.scalar.copy)
 
-        z = keep.tile([P, 4 * V], BF16, name="z", align_bytes=64)
+        z = keep.tile([P, 4 * (V - P)], BF16, name="z", align_bytes=64)
+
+        def z_cols(a, b):
+            return z[:, 4 * (a % (V - P)) : 4 * (a % (V - P) + b - a)]
+
         out_rows = out.rearrange("(a p) v -> p a v", p=P)
 
         def fetch_left(t, a, b):
@@ -139,7 +148,7 @@ def tile_picked_phpair_abs_p_kernel(
 
         def take_abs(a, b):
             nc.scalar.activation(
-                z[:, 4 * a : 4 * b].rearrange("p (v t) -> p v t", t=4), diff[:, :, a:b].rearrange("p t v -> p v t"), ABS
+                z_cols(a, b).rearrange("p (v t) -> p v t", t=4), diff[:, :, a:b].rearrange("p t v -> p v t"), ABS
             )
 
         zw = [keep.tile([P, b - a], U32, name="zw%d" % a, align_bytes=64) for a, b in CHUNKS]
@@ -162,42 +171,49 @@ def tile_picked_phpair_abs_p_kernel(
         diff = keep.tile([P, 4, V], F32, name="diff", align_bytes=64)
         for t in (0, 1):
             fetch_left(t, 0, V)
-        project(3, 0, BANK, 3, nc.scalar.copy)
         project(3, BANK, S, 4, nc.vector.tensor_copy)
+        project(3, 0, BANK, 3, nc.scalar.copy)
         fetch_right(0, 0, V)
         for a in (0, half_pairs):
             for t in (2, 3):
                 fetch_left(t, a, a + half_pairs)
+        def quantise(c):
+            a, b = CHUNKS[c]
+            for u in range(0, b - a, P):
+                nc.vector.quantize_mx(
+                    out=zw[c][:, u : u + P].bitcast(FP8X4), scales=zs[c][:, u : u + P], in_=z_cols(a + u, a + u + P)
+                )
+
         for a, b in CHUNKS:
             if a % half_pairs == 0:
                 for t in (1, 2):
                     fetch_right(t, a, a + half_pairs)
             fetch_right(3, a, b)
-            take_abs(a, min(b, V - ON_VECTOR))
+        for a, b in CHUNKS[:2]:
+            take_abs(a, b)
+        quantise(0)
+        take_abs(V - P, V - ON_VECTOR)
         last = diff[:, :, V - ON_VECTOR : V].rearrange("p t v -> p v t")
         nc.vector.scalar_tensor_tensor(
-            z[:, 4 * (V - ON_VECTOR) : 4 * V].rearrange("p (v t) -> p v t", t=4), last, -1.0, last, MULT, MAX
+            z_cols(V - ON_VECTOR, V).rearrange("p (v t) -> p v t", t=4), last, -1.0, last, MULT, MAX
         )
 
-        for c, (a, b) in enumerate(CHUNKS):
-            for u in range(0, b - a, P):
-                nc.vector.quantize_mx(
-                    out=zw[c][:, u : u + P].bitcast(FP8X4), scales=zs[c][:, u : u + P], in_=z[:, 4 * (a + u) : 4 * (a + u + P)]
-                )
+        for c in (1, 2):
+            quantise(c)
 
-        copies = (nc.scalar.copy, nc.vector.tensor_copy)
-        for m, copy in enumerate(copies):
+        early = keep.tile([P, 2, half_pairs], F32, name="early", tag="diff", align_bytes=64)
+        late = keep.tile([P, 2, half_pairs], F32, name="late", tag="z", align_bytes=64)
+        for m in range(2):
             res = psum.tile([P, half_pairs], F32, name="res", tag="bank%d" % (1 + m))
             second_product(res[:], 0, m)
-            early = keep.tile([P, half_pairs], F32, name="early%d" % m)
-            copy(early[:], res[:])
-            nc.sync.dma_start(out_rows[:, m, 0:half_pairs], early[:])
-        late = [keep.tile([P, half_pairs], F32, name="late%d" % m) for m in range(2)]
+            nc.scalar.copy(early[:, m, :], res[:])
+            nc.sync.dma_start(out_rows[:, m, 0:half_pairs], early[:, m, :])
         for c, banks in ((1, (3, 4)), (2, (6, 7))):
             a, b = CHUNKS[c]
-            for m, copy in enumerate(copies):
+            for m in range(2):
                 res = psum.tile([P, b - a], F32, name="res", tag="bank%d" % banks[m])
                 second_product(res[:], c, m)
-                copy(late[m][:, a - half_pairs : b - half_pairs], res[:])
-        for m, queue in enumerate((nc.scalar, nc.sync)):
-            queue.dma_start(out_rows[:, m, half_pairs:V], late[m][:])
+                copy = nc.scalar.copy if (c, m) == (2, 1) else nc.vector.tensor_copy
+                copy(late[:, m, a - half_pairs : b - half_pairs], res[:])
+        for m, queue in enumerate((nc.sync, nc.scalar)):
+            queue.dma_start(out_rows[:, m, half_pairs:V], late[:, m, :])

@@ -21,12 +21,15 @@ MAX = mybir.AluOpType.max
 P = 128
 BANK = 512
 QUARTER = S // 4
-ON_VECTOR = 64
+HALF_PAIRS = V // 2
+LINE = 4
 
 CHUNKS = [(0, 256), (256, 384), (384, 512)]
 
 TILE0_PIECES = [(0, 256), (256, 512), (512, 768), (768, 896), (896, 1024)]
 TILE0_ON_VECTOR = (1, 3)
+
+ABS_ON_VECTOR = 64
 
 
 def tile_picked_phpair_abs_p_kernel(
@@ -67,23 +70,22 @@ def tile_picked_phpair_abs_p_kernel(
         for r in range(4):
             nc.scalar.dma_start(xs[r:P:32, :].bitcast(I32), xs_picked[8 * r : P : 32, :].bitcast(I32))
 
-        xw = keep.tile([P, S - QUARTER], U32, name="xw", align_bytes=64)
-        nc.vector.tensor_copy(xw[:], xw_all[:].indirect(offs_sb[:, 0 : (S - QUARTER) // 16]))
+        xw = keep.tile([P, S], U32, name="xw", align_bytes=64)
+        nc.vector.tensor_copy(xw[:], xw_all[:].indirect(offs_sb[:]))
 
-        w1_bf = [keep.tile([P, n * P * 4], BF16, name="w1_bf%d" % u, align_bytes=64) for u, n in enumerate((1, 1, 2))]
+        w1_bf = [keep.tile([P, 2 * P * 4], BF16, name="w1_bf%d" % pair, align_bytes=64) for pair in range(2)]
 
-        def cast(copy, u, t0, t1, j0, j1, m0=0, m1=P):
+        def cast(copy, j0, j1, t0, t1, m0=0, m1=P):
             copy(
-                w1_bf[u][:].rearrange("p (t m j) -> p m t j", t=t1 - t0, j=4)[:, m0:m1, :, j0:j1],
+                w1_bf[t0 // 2][:].rearrange("p (t m j) -> p m t j", t=2, j=4)[:, m0:m1, t0 % 2 : t0 % 2 + t1 - t0, j0:j1],
                 w1_raw[:].rearrange("p j (m t) -> p m t j", t=4)[:, m0:m1, t0:t1, j0:j1],
             )
 
-        for t in (0, 1):
-            cast(nc.scalar.copy, t, t, t + 1, 0, 2)
-        cast(nc.scalar.copy, 0, 0, 1, 2, 4, 0, P // 2)
-        cast(nc.vector.tensor_copy, 0, 0, 1, 2, 4, P // 2, P)
-        cast(nc.vector.tensor_copy, 1, 1, 2, 2, 4)
-        cast(nc.scalar.copy, 2, 2, 4, 0, 4)
+        cast(nc.scalar.copy, 0, 2, 0, 2)
+        cast(nc.scalar.copy, 2, 4, 0, 1, 0, P // 2)
+        cast(nc.vector.tensor_copy, 2, 4, 0, 1, P // 2, P)
+        cast(nc.vector.tensor_copy, 2, 4, 1, 2)
+        cast(nc.scalar.copy, 0, 4, 2, 4)
 
         w2w = keep.tile([P, N], U32, name="w2w", tag="w1_raw", align_bytes=64)
         nc.sync.dma_start(w2w[:].bitcast(I32), w2_words[0].rearrange("p n t -> p (n t)").bitcast(I32))
@@ -102,34 +104,30 @@ def tile_picked_phpair_abs_p_kernel(
         w1s = w1s + [w1s_late[:, 0:P], w1s_late[:, P : 2 * P]]
         h = [keep.tile([P, S], F32, name="h%d" % t) for t in range(4)]
 
-        xw_last = keep.tile([P, QUARTER], U32, name="xw_last", tag="w1_bf0", align_bytes=64)
-
         def project(t, a, b, bank, copy):
             acc = psum.tile([P, b - a], F32, name="acc", tag="bank%d" % bank)
-            edge = S - QUARTER
-            for c, d in ((a, min(b, edge)), (max(a, edge), b)):
-                if c < d:
-                    nc.tensor.matmul_mx(
-                        out=acc[:, c - a : d - a],
-                        lhsT=w1w[t].bitcast(FP8X4),
-                        lhsT_scale=w1s[t],
-                        rhs=(xw[:, c:d] if c < edge else xw_last[:, c - edge : d - edge]).bitcast(FP8X4),
-                        rhs_scale=xs[:, c:d],
-                        start=True,
-                        stop=True,
-                    )
+            nc.tensor.matmul_mx(
+                out=acc[:],
+                lhsT=w1w[t].bitcast(FP8X4),
+                lhsT_scale=w1s[t],
+                rhs=xw[:, a:b].bitcast(FP8X4),
+                rhs_scale=xs[:, a:b],
+                start=True,
+                stop=True,
+            )
             copy(h[t][:, a:b], acc[:])
 
-        nc.vector.quantize_mx(out=w1w[0].bitcast(FP8X4), scales=w1s[0], in_=w1_bf[0][:])
-        nc.vector.tensor_copy(xw_last[:], xw_all[:].indirect(offs_sb[:, (S - QUARTER) // 16 : S // 16]))
-        nc.vector.quantize_mx(out=w1w[1].bitcast(FP8X4), scales=w1s[1], in_=w1_bf[1][:])
+        for t in range(2):
+            nc.vector.quantize_mx(
+                out=w1w[t].bitcast(FP8X4), scales=w1s[t], in_=w1_bf[0][:, t * 4 * P : (t + 1) * 4 * P]
+            )
         for bank, (a, b) in enumerate(TILE0_PIECES):
             project(0, a, b, bank, nc.vector.tensor_copy if bank in TILE0_ON_VECTOR else nc.scalar.copy)
-        nc.vector.quantize_mx(out=w1w_late[:].bitcast(FP8X4), scales=w1s_late[:], in_=w1_bf[2][:])
+        nc.vector.quantize_mx(out=w1w_late[:].bitcast(FP8X4), scales=w1s_late[:], in_=w1_bf[1][:])
         for u, bank in enumerate((5, 6, 7, 0)):
             project(1, QUARTER * u, QUARTER * (u + 1), bank, nc.vector.tensor_copy)
-        project(2, BANK, S, 2, nc.vector.tensor_copy)
         project(2, 0, BANK, 1, nc.scalar.copy)
+        project(2, BANK, S, 2, nc.vector.tensor_copy)
 
         z = keep.tile([P, 4 * (V - P)], BF16, name="z", align_bytes=64)
 
@@ -146,13 +144,24 @@ def tile_picked_phpair_abs_p_kernel(
                 diff[:, t, a:b], h[t][:].indirect(right_sb[:, a // 16 : b // 16]), lefts[t][:, a:b], SUB
             )
 
-        def take_abs(a, b):
+        def abs_on_scalar(a, b):
             nc.scalar.activation(
-                z_cols(a, b).rearrange("p (v t) -> p v t", t=4), diff[:, :, a:b].rearrange("p t v -> p v t"), ABS
+                z_cols(a, b).rearrange("p (c i t) -> p c t i", i=LINE, t=4),
+                diff[:, :, a:b].rearrange("p t (c i) -> p c t i", i=LINE),
+                ABS,
             )
+
+        def abs_on_vector(a, b):
+            d = diff[:, :, a:b].rearrange("p t v -> p v t")
+            nc.vector.scalar_tensor_tensor(z_cols(a, b).rearrange("p (v t) -> p v t", t=4), d, -1.0, d, MULT, MAX)
 
         zw = [keep.tile([P, b - a], U32, name="zw%d" % a, align_bytes=64) for a, b in CHUNKS]
         zs = [keep.tile([P, b - a], U8, name="zs%d" % a, align_bytes=64) for a, b in CHUNKS]
+
+        def quantise(c):
+            a, b = CHUNKS[c]
+            for u in range(0, b - a, P):
+                nc.vector.quantize_mx(out=zw[c][:, u : u + P].bitcast(FP8X4), scales=zs[c][:, u : u + P], in_=z_cols(a + u, a + u + P))
 
         def second_product(res, c, m):
             for u in range(0, CHUNKS[c][1] - CHUNKS[c][0], P):
@@ -166,54 +175,42 @@ def tile_picked_phpair_abs_p_kernel(
                     stop=True,
                 )
 
-        half_pairs = V // 2
         lefts = [keep.tile([P, V], F32, name="left%d" % t) for t in range(4)]
         diff = keep.tile([P, 4, V], F32, name="diff", align_bytes=64)
         for t in (0, 1):
             fetch_left(t, 0, V)
-        project(3, BANK, S, 4, nc.vector.tensor_copy)
         project(3, 0, BANK, 3, nc.scalar.copy)
+        project(3, BANK, S, 4, nc.vector.tensor_copy)
         fetch_right(0, 0, V)
-        for a in (0, half_pairs):
+        for a in (0, HALF_PAIRS):
             for t in (2, 3):
-                fetch_left(t, a, a + half_pairs)
-        def quantise(c):
-            a, b = CHUNKS[c]
-            for u in range(0, b - a, P):
-                nc.vector.quantize_mx(
-                    out=zw[c][:, u : u + P].bitcast(FP8X4), scales=zs[c][:, u : u + P], in_=z_cols(a + u, a + u + P)
-                )
-
+                fetch_left(t, a, a + HALF_PAIRS)
         for a, b in CHUNKS:
-            if a % half_pairs == 0:
+            if a % HALF_PAIRS == 0:
                 for t in (1, 2):
-                    fetch_right(t, a, a + half_pairs)
+                    fetch_right(t, a, a + HALF_PAIRS)
             fetch_right(3, a, b)
         for a, b in CHUNKS[:2]:
-            take_abs(a, b)
+            abs_on_scalar(a, b)
         quantise(0)
-        take_abs(V - P, V - ON_VECTOR)
-        last = diff[:, :, V - ON_VECTOR : V].rearrange("p t v -> p v t")
-        nc.vector.scalar_tensor_tensor(
-            z_cols(V - ON_VECTOR, V).rearrange("p (v t) -> p v t", t=4), last, -1.0, last, MULT, MAX
-        )
-
+        abs_on_scalar(V - P, V - ABS_ON_VECTOR)
+        abs_on_vector(V - ABS_ON_VECTOR, V)
         for c in (1, 2):
             quantise(c)
 
-        early = keep.tile([P, 2, half_pairs], F32, name="early", tag="diff", align_bytes=64)
-        late = keep.tile([P, 2, half_pairs], F32, name="late", tag="z", align_bytes=64)
+        early = keep.tile([P, 2, HALF_PAIRS], F32, name="early", tag="diff", align_bytes=64)
+        late = keep.tile([P, 2, HALF_PAIRS], F32, name="late", tag="z", align_bytes=64)
         for m in range(2):
-            res = psum.tile([P, half_pairs], F32, name="res", tag="bank%d" % (1 + m))
+            res = psum.tile([P, HALF_PAIRS], F32, name="res", tag="bank%d" % (1 + m))
             second_product(res[:], 0, m)
             nc.scalar.copy(early[:, m, :], res[:])
-            nc.sync.dma_start(out_rows[:, m, 0:half_pairs], early[:, m, :])
+            nc.sync.dma_start(out_rows[:, m, 0:HALF_PAIRS], early[:, m, :])
         for c, banks in ((1, (3, 4)), (2, (6, 7))):
             a, b = CHUNKS[c]
             for m in range(2):
                 res = psum.tile([P, b - a], F32, name="res", tag="bank%d" % banks[m])
                 second_product(res[:], c, m)
                 copy = nc.scalar.copy if (c, m) == (2, 1) else nc.vector.tensor_copy
-                copy(late[:, m, a - half_pairs : b - half_pairs], res[:])
+                copy(late[:, m, a - HALF_PAIRS : b - HALF_PAIRS], res[:])
         for m, queue in enumerate((nc.sync, nc.scalar)):
-            queue.dma_start(out_rows[:, m, half_pairs:V], late[:, m, :])
+            queue.dma_start(out_rows[:, m, HALF_PAIRS:V], late[:, m, :])

@@ -19,17 +19,8 @@ MULT = mybir.AluOpType.mult
 MAX = mybir.AluOpType.max
 
 P = 128
-BANK = 512
-QUARTER = S // 4
-HALF_PAIRS = V // 2
 LINE = 4
-
-CHUNKS = [(0, 256), (256, 384), (384, 512)]
-
-TILE0_PIECES = [(0, 256), (256, 512), (512, 768), (768, 896), (896, 1024)]
-TILE0_ON_VECTOR = (1, 3)
-
-ABS_ON_VECTOR = 64
+EARLY = 768
 
 
 def tile_picked_phpair_abs_p_kernel(
@@ -38,21 +29,23 @@ def tile_picked_phpair_abs_p_kernel(
     nc = tc.nc
     with ExitStack() as ctx:
         keep = ctx.enter_context(tc.tile_pool(name="keep", bufs=1))
+        shared = ctx.enter_context(tc.tile_pool(name="shared", bufs=1))
         psum = ctx.enter_context(tc.psum_pool(name="psum", bufs=1))
+
+        def sb(name, cols, dtype, tag=None):
+            return keep.tile([P, cols], dtype, name=name, tag=tag or name, align_bytes=64)
 
         offs_sb = keep.tile([P, S // 16], U16, name="offs_sb")
         left_sb = keep.tile([P, V // 16], U16, name="left_sb")
         right_sb = keep.tile([P, V // 16], U16, name="right_sb")
 
         nc.sync.dma_start(offs_sb[:], offs)
-        xs_all = keep.tile([P, T], U8, name="xs_all", align_bytes=64)
-        nc.scalar.dma_start(
-            xs_all[:].bitcast(I32), x_scales[0].bitcast(I32).unsqueeze(1).to_broadcast([16, 8, T // 4])
-        )
-        xw_all = keep.tile([P, T], U32, name="xw_all", align_bytes=64)
+        xs_all = sb("xs_all", T, U8)
+        nc.scalar.dma_start(xs_all[:].bitcast(I32), x_scales[0].bitcast(I32).unsqueeze(1).to_broadcast([16, 8, T // 4]))
+        xw_all = shared.tile([P, T], U32, name="xw_all", offset=0, align_bytes=64)
         nc.sync.dma_start(xw_all[:].bitcast(I32), x_words[0].rearrange("p n t -> p (n t)").bitcast(I32))
         w1_rows = w1.rearrange("(p j) c -> p j c", j=4)
-        w1_raw = keep.tile([P, 4, H], F32, name="w1_raw", align_bytes=64)
+        w1_raw = keep.tile([P, 4, H], F32, name="w1_raw", tag="w1_raw", align_bytes=64)
         for half in range(2):
             nc.sync.dma_start(w1_raw[:, 2 * half : 2 * half + 2, :], w1_rows[:, 2 * half : 2 * half + 2, :])
         nc.sync.dma_start(left_sb[:], left)
@@ -62,155 +55,160 @@ def tile_picked_phpair_abs_p_kernel(
         nc.vector.memset(warm[:, 0:1], 0.0)
         nc.scalar.activation(warm[:, 1:2], warm[:, 0:1], ABS)
 
-        xs = keep.tile([P, S], U8, name="xs", align_bytes=64)
+        xs = sb("xs", S, U8)
         nc.vector.memset(xs[:].bitcast(I32), 0)
-
-        xs_picked = keep.tile([P, S], U8, name="xs_picked", align_bytes=64)
+        xs_picked = sb("xs_picked", S, U8)
         nc.vector.tensor_copy(xs_picked[:], xs_all[:].indirect(offs_sb[:]))
         for r in range(4):
-            nc.scalar.dma_start(xs[r:P:32, :].bitcast(I32), xs_picked[8 * r : P : 32, :].bitcast(I32))
+            (nc.sync if r % 2 else nc.scalar).dma_start(xs[r:P:32, :].bitcast(I32), xs_picked[8 * r : P : 32, :].bitcast(I32))
+        xw = sb("xw", EARLY, U32)
+        nc.vector.tensor_copy(xw[:], xw_all[:].indirect(offs_sb[:, 0 : EARLY // 16]))
 
-        xw = keep.tile([P, S], U32, name="xw", align_bytes=64)
-        nc.vector.tensor_copy(xw[:], xw_all[:].indirect(offs_sb[:]))
-
-        w1_bf = [keep.tile([P, 2 * P * 4], BF16, name="w1_bf%d" % pair, align_bytes=64) for pair in range(2)]
+        w1_bf = sb("w1_bf", 16 * P, BF16)
+        place = (0, 1, 2, 3)
 
         def cast(copy, j0, j1, t0, t1, m0=0, m1=P):
             copy(
-                w1_bf[t0 // 2][:].rearrange("p (t m j) -> p m t j", t=2, j=4)[:, m0:m1, t0 % 2 : t0 % 2 + t1 - t0, j0:j1],
+                w1_bf[:].rearrange("p (u m j) -> p m u j", u=4, j=4)[:, m0:m1, place[t0] : place[t0] + t1 - t0, j0:j1],
                 w1_raw[:].rearrange("p j (m t) -> p m t j", t=4)[:, m0:m1, t0:t1, j0:j1],
             )
 
-        cast(nc.scalar.copy, 0, 2, 0, 2)
-        cast(nc.scalar.copy, 2, 4, 0, 1, 0, P // 2)
-        cast(nc.vector.tensor_copy, 2, 4, 0, 1, P // 2, P)
-        cast(nc.vector.tensor_copy, 2, 4, 1, 2)
-        cast(nc.scalar.copy, 0, 4, 2, 4)
+        w1w = sb("w1w", 4 * P, U32)
+        w1s_first = sb("w1s_first", P, U8)
+        w1s_rest = shared.tile([P, 3 * P], U8, name="w1s_rest", offset=4 * S, align_bytes=64)
+        w1s = [w1s_rest[:, 0:P], w1s_first[:], w1s_rest[:, P : 3 * P]]
 
-        w2w = keep.tile([P, N], U32, name="w2w", tag="w1_raw", align_bytes=64)
+        def stationary(t):
+            scales = w1s[t] if t < 2 else w1s_rest[:, (t - 1) * P : t * P]
+            return w1w[:, t * P : (t + 1) * P].bitcast(FP8X4), scales
+
+        cast(nc.scalar.copy, 0, 2, 0, 2)
+        cast(nc.gpsimd.tensor_copy, 0, 2, 2, 4)
+        cast(nc.scalar.copy, 2, 4, 1, 2, 0, P // 2)
+        cast(nc.vector.tensor_copy, 2, 4, 1, 2, P // 2, P)
+        cast(nc.vector.tensor_copy, 2, 4, 0, 1)
+        nc.vector.quantize_mx(out=stationary(1)[0], scales=w1s[1], in_=w1_bf[:, 4 * P : 8 * P])
+        xw_late = sb("xw_late", S - EARLY, U32, tag="xs_picked")
+        nc.vector.tensor_copy(xw_late[:], xw_all[:].indirect(offs_sb[:, EARLY // 16 : S // 16]))
+        nc.vector.quantize_mx(out=stationary(0)[0], scales=w1s[0], in_=w1_bf[:, 0 : 4 * P])
+        cast(nc.scalar.copy, 2, 4, 2, 4)
+
+        h = [
+            shared.tile([P, S], F32, name="h1", offset=0, align_bytes=64) if t == 1 else keep.tile([P, S], F32, name="h%d" % t)
+            for t in range(4)
+        ]
+
+        def project(t, a, b, bank, copy):
+            acc = psum.tile([P, b - a], F32, name="acc", tag="bank%d" % bank)
+            words, scales = stationary(t)
+            for lo, hi in ((a, EARLY), (EARLY, b)) if a < EARLY < b else ((a, b),):
+                picked = xw[:, lo:hi] if lo < EARLY else xw_late[:, lo - EARLY : hi - EARLY]
+                nc.tensor.matmul_mx(
+                    out=acc[:, lo - a : hi - a], lhsT=words, lhsT_scale=scales, rhs=picked.bitcast(FP8X4),
+                    rhs_scale=xs[:, lo:hi], start=True, stop=True,
+                )
+            copy(h[t][:, a:b], acc[:])
+
+        on_s, on_v = nc.scalar.copy, nc.vector.tensor_copy
+        for bank, (a, b, copy) in enumerate(
+            [(0, 256, on_s), (256, 512, on_v), (512, 768, on_s), (768, 896, on_v), (896, 1024, on_s)]
+        ):
+            project(1, a, b, bank, copy)
+        nc.vector.quantize_mx(out=w1w[:, 2 * P : 4 * P].bitcast(FP8X4), scales=w1s[2], in_=w1_bf[:, 8 * P : 16 * P])
+        w2w = sb("w2w", N, U32, tag="w1_raw")
         nc.sync.dma_start(w2w[:].bitcast(I32), w2_words[0].rearrange("p n t -> p (n t)").bitcast(I32))
-        w2s = keep.tile([P, N], U8, name="w2s", tag="xs_picked", align_bytes=64)
+        w2s = sb("w2s", N, U8, tag="w1_bf")
         for q in range(4):
             nc.sync.dma_start(
                 w2s[32 * q : 32 * q + 32, :].bitcast(I32),
                 w2_scales[0, 4 * q : 4 * q + 4, :].bitcast(I32).unsqueeze(0).to_broadcast([8, 4, N // 4]),
             )
 
-        w1w_late = keep.tile([P, 2 * P], U32, name="w1w_late", align_bytes=64)
-        w1s_late = keep.tile([P, 2 * P], U8, name="w1s_late", align_bytes=64)
-        w1w = [keep.tile([P, P], U32, name="w1w%d" % t, align_bytes=64)[:] for t in range(2)]
-        w1s = [keep.tile([P, P], U8, name="w1s%d" % t, align_bytes=64)[:] for t in range(2)]
-        w1w = w1w + [w1w_late[:, 0:P], w1w_late[:, P : 2 * P]]
-        w1s = w1s + [w1s_late[:, 0:P], w1s_late[:, P : 2 * P]]
-        h = [keep.tile([P, S], F32, name="h%d" % t) for t in range(4)]
+        for bank, a, b in ((5, 0, 256), (6, 256, 512), (7, 512, 1024)):
+            project(0, a, b, bank, on_s)
+        for t in (2, 3):
+            for u in range(2):
+                project(t, 512 * u, 512 * u + (128 if (t, u) == (3, 1) else 512), 2 * t - 4 + u, on_s)
 
-        def project(t, a, b, bank, copy):
-            acc = psum.tile([P, b - a], F32, name="acc", tag="bank%d" % bank)
-            nc.tensor.matmul_mx(
-                out=acc[:],
-                lhsT=w1w[t].bitcast(FP8X4),
-                lhsT_scale=w1s[t],
-                rhs=xw[:, a:b].bitcast(FP8X4),
-                rhs_scale=xs[:, a:b],
-                start=True,
-                stop=True,
-            )
-            copy(h[t][:, a:b], acc[:])
-
-        for t in range(2):
-            nc.vector.quantize_mx(
-                out=w1w[t].bitcast(FP8X4), scales=w1s[t], in_=w1_bf[0][:, t * 4 * P : (t + 1) * 4 * P]
-            )
-        for bank, (a, b) in enumerate(TILE0_PIECES):
-            project(0, a, b, bank, nc.vector.tensor_copy if bank in TILE0_ON_VECTOR else nc.scalar.copy)
-        nc.vector.quantize_mx(out=w1w_late[:].bitcast(FP8X4), scales=w1s_late[:], in_=w1_bf[1][:])
-        for u, bank in enumerate((5, 6, 7, 0)):
-            project(1, QUARTER * u, QUARTER * (u + 1), bank, nc.vector.tensor_copy)
-        project(2, 0, BANK, 1, nc.scalar.copy)
-        project(2, BANK, S, 2, nc.vector.tensor_copy)
-
-        z = keep.tile([P, 4 * (V - P)], BF16, name="z", align_bytes=64)
-
-        def z_cols(a, b):
-            return z[:, 4 * (a % (V - P)) : 4 * (a % (V - P) + b - a)]
-
+        lefts = [keep.tile([P, V], F32, name="left%d" % t, align_bytes=64) for t in range(4)]
+        diff = keep.tile([P, 4, V], F32, name="diff", tag="xs_picked", align_bytes=64)
+        z = sb("z", 4 * (V - P), BF16)
         out_rows = out.rearrange("(a p) v -> p a v", p=P)
 
-        def fetch_left(t, a, b):
-            nc.scalar.activation(lefts[t][:, a:b], h[t][:].indirect(left_sb[:, a // 16 : b // 16]), COPY)
+        def z_cols(a, b):
+            back = 256 if a >= 384 else 0
+            return z[:, 4 * (a - back) : 4 * (b - back)]
 
-        def fetch_right(t, a, b):
-            nc.vector.tensor_tensor(
-                diff[:, t, a:b], h[t][:].indirect(right_sb[:, a // 16 : b // 16]), lefts[t][:, a:b], SUB
-            )
+        def left_cols(t, a, b):
+            return lefts[t][:, 0 : b - a] if (t, a) == (3, 384) else lefts[t][:, a:b]
 
-        def abs_on_scalar(a, b):
+        def left_s(t, a, b):
+            nc.scalar.activation(left_cols(t, a, b), h[t][:].indirect(left_sb[:, a // 16 : b // 16]), COPY)
+
+        def left_v(t, a, b):
+            nc.vector.tensor_copy(lefts[t][:, a:b], h[t][:].indirect(left_sb[:, a // 16 : b // 16]))
+
+        def right_v(t, a, b):
+            nc.vector.tensor_tensor(diff[:, t, a:b], h[t][:].indirect(right_sb[:, a // 16 : b // 16]), left_cols(t, a, b), SUB)
+
+        def abs_s(a, b):
             nc.scalar.activation(
                 z_cols(a, b).rearrange("p (c i t) -> p c t i", i=LINE, t=4),
                 diff[:, :, a:b].rearrange("p t (c i) -> p c t i", i=LINE),
                 ABS,
             )
 
-        def abs_on_vector(a, b):
+        def abs_v(a, b):
             d = diff[:, :, a:b].rearrange("p t v -> p v t")
             nc.vector.scalar_tensor_tensor(z_cols(a, b).rearrange("p (v t) -> p v t", t=4), d, -1.0, d, MULT, MAX)
 
-        zw = [keep.tile([P, b - a], U32, name="zw%d" % a, align_bytes=64) for a, b in CHUNKS]
-        zs = [keep.tile([P, b - a], U8, name="zs%d" % a, align_bytes=64) for a, b in CHUNKS]
+        zw = [sb("zw%d" % c, P, U32) for c in range(4)]
+        zs = [sb("zs%d" % c, P, U8) for c in range(4)]
 
         def quantise(c):
-            a, b = CHUNKS[c]
-            for u in range(0, b - a, P):
-                nc.vector.quantize_mx(out=zw[c][:, u : u + P].bitcast(FP8X4), scales=zs[c][:, u : u + P], in_=z_cols(a + u, a + u + P))
+            nc.vector.quantize_mx(out=zw[c][:].bitcast(FP8X4), scales=zs[c][:], in_=z_cols(P * c, P * c + P))
 
         def second_product(res, c, m):
-            for u in range(0, CHUNKS[c][1] - CHUNKS[c][0], P):
-                nc.tensor.matmul_mx(
-                    out=res[:, u : u + P],
-                    lhsT=w2w[:, m * P : (m + 1) * P].bitcast(FP8X4),
-                    lhsT_scale=w2s[:, m * P : (m + 1) * P],
-                    rhs=zw[c][:, u : u + P].bitcast(FP8X4),
-                    rhs_scale=zs[c][:, u : u + P],
-                    start=True,
-                    stop=True,
-                )
+            nc.tensor.matmul_mx(
+                out=res, lhsT=w2w[:, m * P : (m + 1) * P].bitcast(FP8X4), lhsT_scale=w2s[:, m * P : (m + 1) * P],
+                rhs=zw[c][:].bitcast(FP8X4), rhs_scale=zs[c][:], start=True, stop=True,
+            )
 
-        lefts = [keep.tile([P, V], F32, name="left%d" % t) for t in range(4)]
-        diff = keep.tile([P, 4, V], F32, name="diff", align_bytes=64)
-        for t in (0, 1):
-            fetch_left(t, 0, V)
-        project(3, 0, BANK, 3, nc.scalar.copy)
-        project(3, BANK, S, 4, nc.vector.tensor_copy)
-        fetch_right(0, 0, V)
-        for a in (0, HALF_PAIRS):
-            for t in (2, 3):
-                fetch_left(t, a, a + HALF_PAIRS)
-        for a, b in CHUNKS:
-            if a % HALF_PAIRS == 0:
-                for t in (1, 2):
-                    fetch_right(t, a, a + HALF_PAIRS)
-            fetch_right(3, a, b)
-        for a, b in CHUNKS[:2]:
-            abs_on_scalar(a, b)
+        left_v(1, 0, V)
+        project(3, 640, 1024, 7, on_v)
+        left_v(0, 0, 256)
+        for t, a, b in ((2, 0, 256), (3, 0, 256), (0, 256, 512), (2, 256, 512), (3, 256, 384)):
+            left_s(t, a, b)
+        right_v(1, 0, V)
+        for t in (0, 2, 3):
+            right_v(t, 0, 256)
+        for t in (0, 2):
+            right_v(t, 256, 512)
+        right_v(3, 256, 384)
+        abs_s(0, 128)
+        left_s(3, 384, 512)
         quantise(0)
-        abs_on_scalar(V - P, V - ABS_ON_VECTOR)
-        abs_on_vector(V - ABS_ON_VECTOR, V)
-        for c in (1, 2):
-            quantise(c)
+        right_v(3, 384, 512)
+        abs_s(128, 256)
+        abs_s(256, 384)
+        quantise(1)
+        abs_s(384, 448)
+        abs_v(448, 512)
+        quantise(2)
+        quantise(3)
 
-        early = keep.tile([P, 2, HALF_PAIRS], F32, name="early", tag="diff", align_bytes=64)
-        late = keep.tile([P, 2, HALF_PAIRS], F32, name="late", tag="z", align_bytes=64)
+        early = keep.tile([P, 2, 256], F32, name="early", tag="xs_picked", align_bytes=64)
+        late = keep.tile([P, 2, 256], F32, name="late", tag="z", align_bytes=64)
         for m in range(2):
-            res = psum.tile([P, HALF_PAIRS], F32, name="res", tag="bank%d" % (1 + m))
-            second_product(res[:], 0, m)
-            nc.scalar.copy(early[:, m, :], res[:])
-            nc.sync.dma_start(out_rows[:, m, 0:HALF_PAIRS], early[:, m, :])
-        for c, banks in ((1, (3, 4)), (2, (6, 7))):
-            a, b = CHUNKS[c]
+            res = psum.tile([P, 256], F32, name="res", tag="bank%d" % (4 + m))
+            for c in range(2):
+                second_product(res[:, P * c : P * c + P], c, m)
+            on_s(early[:, m, :], res[:])
+            nc.sync.dma_start(out_rows[:, m, 0:256], early[:, m, :])
+        for c, banks in ((2, (6, 0)), (3, (1, 2))):
             for m in range(2):
-                res = psum.tile([P, b - a], F32, name="res", tag="bank%d" % banks[m])
+                res = psum.tile([P, P], F32, name="res", tag="bank%d" % banks[m])
                 second_product(res[:], c, m)
-                copy = nc.scalar.copy if (c, m) == (2, 1) else nc.vector.tensor_copy
-                copy(late[:, m, a - HALF_PAIRS : b - HALF_PAIRS], res[:])
+                (on_s if m else on_v)(late[:, m, P * (c - 2) : P * (c - 1)], res[:])
         for m, queue in enumerate((nc.sync, nc.scalar)):
-            queue.dma_start(out_rows[:, m, HALF_PAIRS:V], late[:, m, :])
+            queue.dma_start(out_rows[:, m, 256:V], late[:, m, :])

@@ -209,6 +209,7 @@ def tile_picked_phpair_abs_p_kernel(
             for m in range(2):
                 res = psum.tile([P, P], F32, name="res", tag="bank%d" % banks[m])
                 second_product(res[:], c, m)
-                (on_s if m else on_v)(late[:, m, P * (c - 2) : P * (c - 1)], res[:])
-        for m, queue in enumerate((nc.sync, nc.scalar)):
-            queue.dma_start(out_rows[:, m, 256:V], late[:, m, :])
+                (on_v if m else on_s)(late[:, m, P * (c - 2) : P * (c - 1)], res[:])
+        nc.sync.dma_start(out_rows[:, 1, 256:384], late[:, 1, 0:P])
+        nc.scalar.dma_start(out_rows[:, 0, 256:V], late[:, 0, :])
+        nc.sync.dma_start(out_rows[:, 1, 384:V], late[:, 1, P : 2 * P])

@@ -203,7 +203,7 @@ def tile_picked_phpair_abs_p_kernel(
             res = psum.tile([P, 256], F32, name="res", tag="bank%d" % (4 + m))
             for c in range(2):
                 second_product(res[:, P * c : P * c + P], c, m)
-            on_s(early[:, m, :], res[:])
+            (on_v if m else on_s)(early[:, m, :], res[:])
             nc.sync.dma_start(out_rows[:, m, 0:256], early[:, m, :])
         for c, banks in ((2, (6, 0)), (3, (1, 2))):
             for m in range(2):

@@ -210,6 +210,6 @@ def tile_picked_phpair_abs_p_kernel(
                 res = psum.tile([P, P], F32, name="res", tag="bank%d" % banks[m])
                 second_product(res[:], c, m)
                 (on_v if m else on_s)(late[:, m, P * (c - 2) : P * (c - 1)], res[:])
-        nc.sync.dma_start(out_rows[:, 1, 256:384], late[:, 1, 0:P])
-        nc.scalar.dma_start(out_rows[:, 0, 256:V], late[:, 0, :])
+        nc.sync.dma_start(out_rows[:, :, 256:384], late[:, :, 0:P])
+        nc.scalar.dma_start(out_rows[:, 0, 384:V], late[:, 0, P : 2 * P])
         nc.sync.dma_start(out_rows[:, 1, 384:V], late[:, 1, P : 2 * P])

@@ -128,7 +128,7 @@ def tile_picked_phpair_abs_p_kernel(
             project(0, a, b, bank, on_s)
         for t in (2, 3):
             for u in range(2):
-                project(t, 512 * u, 512 * u + (128 if (t, u) == (3, 1) else 512), 2 * t - 4 + u, on_s)
+                project(t, 512 * u, 512 * u + (256 if (t, u) == (3, 1) else 512), 2 * t - 4 + u, on_s)
 
         lefts = [keep.tile([P, V], F32, name="left%d" % t, align_bytes=64) for t in range(4)]
         diff = keep.tile([P, 4, V], F32, name="diff", tag="xs_picked", align_bytes=64)
@@ -175,7 +175,7 @@ def tile_picked_phpair_abs_p_kernel(
             )
 
         left_v(1, 0, V)
-        project(3, 640, 1024, 7, on_v)
+        project(3, 768, 1024, 7, on_v)
         left_v(0, 0, 256)
         for t, a, b in ((2, 0, 256), (3, 0, 256), (0, 256, 512), (2, 256, 512), (3, 256, 384)):
             left_s(t, a, b)
@@ -192,8 +192,8 @@ def tile_picked_phpair_abs_p_kernel(
         abs_s(128, 256)
         abs_s(256, 384)
         quantise(1)
-        abs_s(384, 448)
-        abs_v(448, 512)
+        abs_s(384, 464)
+        abs_v(464, 512)
         quantise(2)
         quantise(3)
 

@@ -15,8 +15,6 @@ FP8X4 = mybir.dt.float8_e4m3fn_x4
 ABS = mybir.ActivationFunctionType.Abs
 COPY = mybir.ActivationFunctionType.Copy
 SUB = mybir.AluOpType.subtract
-MULT = mybir.AluOpType.mult
-MAX = mybir.AluOpType.max
 
 P = 128
 LINE = 4
@@ -132,12 +130,11 @@ def tile_picked_phpair_abs_p_kernel(
 
         lefts = [keep.tile([P, V], F32, name="left%d" % t, align_bytes=64) for t in range(4)]
         diff = keep.tile([P, 4, V], F32, name="diff", tag="xs_picked", align_bytes=64)
-        z = sb("z", 4 * (V - P), BF16)
+        z = [sb("z%d" % c, 4 * P, BF16) for c in range(4)]
         out_rows = out.rearrange("(a p) v -> p a v", p=P)
 
         def z_cols(a, b):
-            back = 256 if a >= 384 else 0
-            return z[:, 4 * (a - back) : 4 * (b - back)]
+            return z[a // P][:]
 
         def left_cols(t, a, b):
             return lefts[t][:, 0 : b - a] if (t, a) == (3, 384) else lefts[t][:, a:b]
@@ -157,10 +154,6 @@ def tile_picked_phpair_abs_p_kernel(
                 diff[:, :, a:b].rearrange("p t (c i) -> p c t i", i=LINE),
                 ABS,
             )
-
-        def abs_v(a, b):
-            d = diff[:, :, a:b].rearrange("p t v -> p v t")
-            nc.vector.scalar_tensor_tensor(z_cols(a, b).rearrange("p (v t) -> p v t", t=4), d, -1.0, d, MULT, MAX)
 
         zw = [sb("zw%d" % c, P, U32) for c in range(4)]
         zs = [sb("zs%d" % c, P, U8) for c in range(4)]
@@ -192,19 +185,18 @@ def tile_picked_phpair_abs_p_kernel(
         abs_s(128, 256)
         abs_s(256, 384)
         quantise(1)
-        abs_s(384, 464)
-        abs_v(464, 512)
+        abs_s(384, 512)
         quantise(2)
         quantise(3)
 
-        early = keep.tile([P, 2, 256], F32, name="early", tag="xs_picked", align_bytes=64)
-        late = keep.tile([P, 2, 256], F32, name="late", tag="z", align_bytes=64)
-        for m in range(2):
-            res = psum.tile([P, 256], F32, name="res", tag="bank%d" % (4 + m))
-            for c in range(2):
-                second_product(res[:, P * c : P * c + P], c, m)
-            (on_v if m else on_s)(early[:, m, :], res[:])
-            nc.sync.dma_start(out_rows[:, m, 0:256], early[:, m, :])
+        late = keep.tile([P, 2, 256], F32, name="late", tag="z3", align_bytes=64)
+        for c, tag, copy in ((0, "z1", on_v), (1, "xs_picked", on_s)):
+            early = keep.tile([P, 2, P], F32, name="early%d" % c, tag=tag, align_bytes=64)
+            res = psum.tile([P, 2, P], F32, name="res", tag="bank%d" % (4 + c))
+            for m in range(2):
+                second_product(res[:, m, :], c, m)
+            copy(early[:], res[:])
+            nc.sync.dma_start(out_rows[:, :, P * c : P * c + P], early[:])
         for c, banks in ((2, (6, 0)), (3, (1, 2))):
             for m in range(2):
                 res = psum.tile([P, P], F32, name="res", tag="bank%d" % banks[m])

from contextlib import ExitStack

import concourse.mybir as mybir

K, T, S, H, N, V = 512, 2048, 1024, 512, 256, 512
FLOPS = 2 * K * H * S + 2 * H * N * V

F32 = mybir.dt.float32
BF16 = mybir.dt.bfloat16
I32 = mybir.dt.int32
U32 = mybir.dt.uint32
U16 = mybir.dt.uint16
U8 = mybir.dt.uint8
FP8X4 = mybir.dt.float8_e4m3fn_x4
ABS = mybir.ActivationFunctionType.Abs
COPY = mybir.ActivationFunctionType.Copy
SUB = mybir.AluOpType.subtract

P = 128
LINE = 4
EARLY = 768


def tile_picked_phpair_abs_p_kernel(
    tc, x_words, x_scales, w1, w2_words, w2_scales, offs, left, right, out
):
    nc = tc.nc
    with ExitStack() as ctx:
        keep = ctx.enter_context(tc.tile_pool(name="keep", bufs=1))
        shared = ctx.enter_context(tc.tile_pool(name="shared", bufs=1))
        psum = ctx.enter_context(tc.psum_pool(name="psum", bufs=1))

        def sb(name, cols, dtype, tag=None):
            return keep.tile([P, cols], dtype, name=name, tag=tag or name, align_bytes=64)

        offs_sb = keep.tile([P, S // 16], U16, name="offs_sb")
        left_sb = keep.tile([P, V // 16], U16, name="left_sb")
        right_sb = keep.tile([P, V // 16], U16, name="right_sb")

        nc.sync.dma_start(offs_sb[:], offs)
        xs_all = sb("xs_all", T, U8)
        nc.scalar.dma_start(xs_all[:].bitcast(I32), x_scales[0].bitcast(I32).unsqueeze(1).to_broadcast([16, 8, T // 4]))
        xw_all = shared.tile([P, T], U32, name="xw_all", offset=0, align_bytes=64)
        nc.sync.dma_start(xw_all[:].bitcast(I32), x_words[0].rearrange("p n t -> p (n t)").bitcast(I32))
        w1_rows = w1.rearrange("(p j) c -> p j c", j=4)
        w1_raw = keep.tile([P, 4, H], F32, name="w1_raw", tag="w1_raw", align_bytes=64)
        for half in range(2):
            nc.sync.dma_start(w1_raw[:, 2 * half : 2 * half + 2, :], w1_rows[:, 2 * half : 2 * half + 2, :])
        nc.sync.dma_start(left_sb[:], left)
        nc.sync.dma_start(right_sb[:], right)

        warm = keep.tile([P, 2], F32, name="warm")
        nc.vector.memset(warm[:, 0:1], 0.0)
        nc.scalar.activation(warm[:, 1:2], warm[:, 0:1], ABS)

        xs = sb("xs", S, U8)
        nc.vector.memset(xs[:].bitcast(I32), 0)
        xs_picked = sb("xs_picked", S, U8)
        nc.vector.tensor_copy(xs_picked[:], xs_all[:].indirect(offs_sb[:]))
        for r in range(4):
            (nc.sync if r % 2 else nc.scalar).dma_start(xs[r:P:32, :].bitcast(I32), xs_picked[8 * r : P : 32, :].bitcast(I32))
        xw = sb("xw", EARLY, U32)
        nc.vector.tensor_copy(xw[:], xw_all[:].indirect(offs_sb[:, 0 : EARLY // 16]))

        w1_bf = sb("w1_bf", 16 * P, BF16)
        place = (0, 1, 2, 3)

        def cast(copy, j0, j1, t0, t1, m0=0, m1=P):
            copy(
                w1_bf[:].rearrange("p (u m j) -> p m u j", u=4, j=4)[:, m0:m1, place[t0] : place[t0] + t1 - t0, j0:j1],
                w1_raw[:].rearrange("p j (m t) -> p m t j", t=4)[:, m0:m1, t0:t1, j0:j1],
            )

        w1w = sb("w1w", 4 * P, U32)
        w1s_first = sb("w1s_first", P, U8)
        w1s_rest = shared.tile([P, 3 * P], U8, name="w1s_rest", offset=4 * S, align_bytes=64)
        w1s = [w1s_rest[:, 0:P], w1s_first[:], w1s_rest[:, P : 3 * P]]

        def stationary(t):
            scales = w1s[t] if t < 2 else w1s_rest[:, (t - 1) * P : t * P]
            return w1w[:, t * P : (t + 1) * P].bitcast(FP8X4), scales

        cast(nc.scalar.copy, 0, 2, 0, 2)
        cast(nc.gpsimd.tensor_copy, 0, 2, 2, 4)
        cast(nc.scalar.copy, 2, 4, 1, 2, 0, P // 2)
        cast(nc.vector.tensor_copy, 2, 4, 1, 2, P // 2, P)
        cast(nc.vector.tensor_copy, 2, 4, 0, 1)
        nc.vector.quantize_mx(out=stationary(1)[0], scales=w1s[1], in_=w1_bf[:, 4 * P : 8 * P])
        xw_late = sb("xw_late", S - EARLY, U32, tag="xs_picked")
        nc.vector.tensor_copy(xw_late[:], xw_all[:].indirect(offs_sb[:, EARLY // 16 : S // 16]))
        nc.vector.quantize_mx(out=stationary(0)[0], scales=w1s[0], in_=w1_bf[:, 0 : 4 * P])
        cast(nc.scalar.copy, 2, 4, 2, 4)

        h = [
            shared.tile([P, S], F32, name="h1", offset=0, align_bytes=64) if t == 1 else keep.tile([P, S], F32, name="h%d" % t)
            for t in range(4)
        ]

        def project(t, a, b, bank, copy):
            acc = psum.tile([P, b - a], F32, name="acc", tag="bank%d" % bank)
            words, scales = stationary(t)
            for lo, hi in ((a, EARLY), (EARLY, b)) if a < EARLY < b else ((a, b),):
                picked = xw[:, lo:hi] if lo < EARLY else xw_late[:, lo - EARLY : hi - EARLY]
                nc.tensor.matmul_mx(
                    out=acc[:, lo - a : hi - a], lhsT=words, lhsT_scale=scales, rhs=picked.bitcast(FP8X4),
                    rhs_scale=xs[:, lo:hi], start=True, stop=True,
                )
            copy(h[t][:, a:b], acc[:])

        on_s, on_v = nc.scalar.copy, nc.vector.tensor_copy
        for bank, (a, b, copy) in enumerate(
            [(0, 256, on_s), (256, 512, on_v), (512, 768, on_s), (768, 896, on_v), (896, 1024, on_s)]
        ):
            project(1, a, b, bank, copy)
        nc.vector.quantize_mx(out=w1w[:, 2 * P : 4 * P].bitcast(FP8X4), scales=w1s[2], in_=w1_bf[:, 8 * P : 16 * P])
        w2w = sb("w2w", N, U32, tag="w1_raw")
        nc.sync.dma_start(w2w[:].bitcast(I32), w2_words[0].rearrange("p n t -> p (n t)").bitcast(I32))
        w2s = sb("w2s", N, U8, tag="w1_bf")
        for q in range(4):
            nc.sync.dma_start(
                w2s[32 * q : 32 * q + 32, :].bitcast(I32),
                w2_scales[0, 4 * q : 4 * q + 4, :].bitcast(I32).unsqueeze(0).to_broadcast([8, 4, N // 4]),
            )

        for bank, a, b in ((5, 0, 256), (6, 256, 512), (7, 512, 1024)):
            project(0, a, b, bank, on_s)
        for t in (2, 3):
            for u in range(2):
                project(t, 512 * u, 512 * u + (256 if (t, u) == (3, 1) else 512), 2 * t - 4 + u, on_s)

        lefts = [keep.tile([P, V], F32, name="left%d" % t, align_bytes=64) for t in range(4)]
        diff = keep.tile([P, 4, V], F32, name="diff", tag="xs_picked", align_bytes=64)
        z = [sb("z%d" % c, 4 * P, BF16) for c in range(4)]
        out_rows = out.rearrange("(a p) v -> p a v", p=P)

        def z_cols(a, b):
            return z[a // P][:]

        def left_cols(t, a, b):
            return lefts[t][:, 0 : b - a] if (t, a) == (3, 384) else lefts[t][:, a:b]

        def left_s(t, a, b):
            nc.scalar.activation(left_cols(t, a, b), h[t][:].indirect(left_sb[:, a // 16 : b // 16]), COPY)

        def left_v(t, a, b):
            nc.vector.tensor_copy(lefts[t][:, a:b], h[t][:].indirect(left_sb[:, a // 16 : b // 16]))

        def right_v(t, a, b):
            nc.vector.tensor_tensor(diff[:, t, a:b], h[t][:].indirect(right_sb[:, a // 16 : b // 16]), left_cols(t, a, b), SUB)

        def abs_s(a, b):
            nc.scalar.activation(
                z_cols(a, b).rearrange("p (c i t) -> p c t i", i=LINE, t=4),
                diff[:, :, a:b].rearrange("p t (c i) -> p c t i", i=LINE),
                ABS,
            )

        zw = [sb("zw%d" % c, P, U32) for c in range(4)]
        zs = [sb("zs%d" % c, P, U8) for c in range(4)]

        def quantise(c):
            nc.vector.quantize_mx(out=zw[c][:].bitcast(FP8X4), scales=zs[c][:], in_=z_cols(P * c, P * c + P))

        def second_product(res, c, m):
            nc.tensor.matmul_mx(
                out=res, lhsT=w2w[:, m * P : (m + 1) * P].bitcast(FP8X4), lhsT_scale=w2s[:, m * P : (m + 1) * P],
                rhs=zw[c][:].bitcast(FP8X4), rhs_scale=zs[c][:], start=True, stop=True,
            )

        left_v(1, 0, V)
        project(3, 768, 1024, 7, on_v)
        left_v(0, 0, 256)
        for t, a, b in ((2, 0, 256), (3, 0, 256), (0, 256, 512), (2, 256, 512), (3, 256, 384)):
            left_s(t, a, b)
        right_v(1, 0, V)
        for t in (0, 2, 3):
            right_v(t, 0, 256)
        for t in (0, 2):
            right_v(t, 256, 512)
        right_v(3, 256, 384)
        abs_s(0, 128)
        left_s(3, 384, 512)
        quantise(0)
        right_v(3, 384, 512)
        abs_s(128, 256)
        abs_s(256, 384)
        quantise(1)
        abs_s(384, 512)
        quantise(2)
        quantise(3)

        late = keep.tile([P, 2, 256], F32, name="late", tag="z3", align_bytes=64)
        for c, tag, copy in ((0, "z1", on_v), (1, "xs_picked", on_s)):
            early = keep.tile([P, 2, P], F32, name="early%d" % c, tag=tag, align_bytes=64)
            res = psum.tile([P, 2, P], F32, name="res", tag="bank%d" % (4 + c))
            for m in range(2):
                second_product(res[:, m, :], c, m)
            copy(early[:], res[:])
            nc.sync.dma_start(out_rows[:, :, P * c : P * c + P], early[:])
        for c, banks in ((2, (6, 0)), (3, (1, 2))):
            for m in range(2):
                res = psum.tile([P, P], F32, name="res", tag="bank%d" % banks[m])
                second_product(res[:], c, m)
                (on_v if m else on_s)(late[:, m, P * (c - 2) : P * (c - 1)], res[:])
        nc.sync.dma_start(out_rows[:, :, 256:384], late[:, :, 0:P])
        nc.scalar.dma_start(out_rows[:, 0, 384:V], late[:, 0, P : 2 * P])
        nc.sync.dma_start(out_rows[:, 1, 384:V], late[:, 1, P : 2 * P])
